import numpy as np
import ml_dtypes


def mxq(x, axis, fmt="e4m3"):
    dtype, down = {"e4m3": (ml_dtypes.float8_e4m3fn, 7), "e5m2": (ml_dtypes.float8_e5m2, 14)}[fmt]
    v = np.moveaxis(np.asarray(x, np.float32).astype(ml_dtypes.bfloat16).astype(np.float64), axis, -1)
    blocks = v.reshape(v.shape[:-1] + (-1, 32))
    amax = np.abs(blocks).max(-1, keepdims=True)
    byte = np.maximum(np.where(amax > 0, np.frexp(amax)[1] - 1 + 127, 0) - down, 1)
    scale = np.exp2(byte - 127.0)
    codes = (blocks / scale).astype(np.float32).astype(dtype).astype(np.float64)
    return np.moveaxis((codes * scale).reshape(v.shape), -1, axis)


WIDE = False


def mx_kscale(k):
    if not WIDE:
        return np.ones(k)
    levels = np.array([10, -10, 5, -5, 0])
    if k % 512:
        return np.exp2(np.random.permutation(np.resize(levels, k // 32))).repeat(32)
    a = np.empty((k // 512, 16))
    for p in range(k // 512):
        a[p, :8] = np.random.permutation(np.resize(levels, 8))
        for g in range(8):
            far = levels[np.abs(levels - a[p, g]) >= 10]
            a[p, g + 8] = far[np.random.randint(len(far))]
    return np.exp2(a.ravel()).repeat(32)


def f64(x):
    return np.asarray(x).astype(np.float64)


def striped(idx):
    return np.tile(idx.reshape(-1, 16).T, (8, 1)).astype(np.uint16)


def unstriped(offs):
    return offs[:16].T.reshape(-1).astype(np.int64)


def pack_weight(w):
    k, n = w.shape
    w = f64(np.asarray(w, np.float32).astype(ml_dtypes.bfloat16)).reshape(k // 32, 32, n)
    amax = np.abs(w).max(1)
    byte = np.clip(np.where(amax > 0, np.frexp(amax)[1] - 1 + 127 - 7, 1), 1, 254)
    scaled = (w * np.exp2(127.0 - byte)[:, None, :]).reshape(k, n).astype(np.float32)
    words = np.ascontiguousarray(scaled.reshape(k // 512, 128, 4, n).transpose(0, 1, 3, 2)).astype(ml_dtypes.float8_e4m3fn).view(np.uint8)
    return words, np.ascontiguousarray(byte.astype(np.uint8).reshape(k // 512, 16, n))


def unpack_weight(words, scales):
    g, p, n, _ = words.shape
    vals = np.ascontiguousarray(words).view(ml_dtypes.float8_e4m3fn).astype(np.float64) * np.repeat(np.exp2(scales.astype(np.float64) - 127.0), 8, axis=1)[..., None]
    return vals.transpose(0, 1, 3, 2).reshape(g * 512, n)

def planes(y):
    n, m = y.shape
    v = y.astype(np.float32).astype(ml_dtypes.bfloat16).astype(np.float64).reshape(n // 32, 32, m)
    top = np.abs(v).max(1)
    byte = np.clip(np.where(top > 0, np.frexp(top)[1] - 1 + 127 - 7, 1), 1, 254)
    codes = (v * np.exp2(127.0 - byte)[:, None, :]).reshape(n, m).astype(np.float32).astype(ml_dtypes.float8_e4m3fn).view(np.uint8)
    words = codes.reshape(n // 512, 128, 4, m).transpose(0, 1, 3, 2)
    return np.ascontiguousarray(words), np.ascontiguousarray(byte.astype(np.uint8).reshape(n // 512, 16, m))


K, T, S, N, U = 512, 1024, 512, 512, 1024


def setup_inputs():
    n = np.random.standard_normal
    s = mx_kscale(K)[:, None]
    packed_xT = pack_weight(n((K, T)) * s)
    return {
        "x_words": packed_xT[0],
        "x_scales": packed_xT[1],
        "mem": n((N, U)).astype(np.float32),
        "w1": (n((K, N)) / np.sqrt(K) / s).astype(np.float32),
        "offs": striped(np.random.permutation(T)[:S]),
        "slot": striped(np.random.permutation(U)[:S]),
    }


def reference(x_words, x_scales, mem, w1, offs, slot):
    xq = unpack_weight(x_words, x_scales)[:, unstriped(offs)]
    y = mxq(f64(w1), 0, "e4m3").T @ xq
    out = f64(mem).copy()
    out[:, unstriped(slot)] = f64(mem)[:, unstriped(slot)] + y
    return (out,) + planes(out)

@@ -1,0 +1,158 @@
+from contextlib import ExitStack
+
+import concourse.mybir as mybir
+
+K, T, S, N, U = 512, 1024, 512, 512, 1024
+FLOPS = 2 * K * N * S
+
+F32 = mybir.dt.float32
+BF16 = mybir.dt.bfloat16
+I32 = mybir.dt.int32
+U32 = mybir.dt.uint32
+U16 = mybir.dt.uint16
+U8 = mybir.dt.uint8
+FP8X4 = mybir.dt.float8_e4m3fn_x4
+ADD = mybir.AluOpType.add
+
+P = 128
+PACK = 4
+CHUNKS = 4
+CW = U // CHUNKS
+
+
+def tile_picked_idxput_add_po_kernel(
+    tc, x_words, x_scales, mem, w1, offs, slot, out_0, out_1, out_2
+):
+    nc = tc.nc
+    with ExitStack() as ctx:
+        keep = ctx.enter_context(tc.tile_pool(name="keep", bufs=1))
+        psum = ctx.enter_context(tc.psum_pool(name="psum", bufs=1))
+
+        offs_t = keep.tile([P, S // 16], U16, name="offs_t")
+        slot_t = keep.tile([P, S // 16], U16, name="slot_t")
+        xw = keep.tile([P, T], I32, name="xw", align_bytes=64)
+        xs = keep.tile([P, T], U8, name="xs", align_bytes=64)
+        w_raw = keep.tile([P, PACK, N], F32, name="w_raw", align_bytes=64)
+        win = [keep.tile([P, U], F32, name="win%d" % t, align_bytes=64) for t in range(PACK)]
+        warm = keep.tile([P, 8], F32, name="warm")
+        warm2 = keep.tile([P, 8], F32, name="warm2")
+
+        mem_rows = mem.rearrange("(p t) u -> p t u", t=PACK)
+        out_rows = out_0.rearrange("(p t) u -> p t u", t=PACK)
+
+        nc.vector.memset(xs[:].bitcast(I32), 0)
+        nc.gpsimd.memset(warm[:], 0.0)
+        nc.sync.dma_start(offs_t[:], offs)
+        nc.sync.dma_start(xw[:], x_words[0].rearrange("p c r -> p (c r)").bitcast(I32))
+        nc.sync.dma_start(slot_t[:], slot)
+        nc.sync.dma_start(win[0][:], mem_rows[:, 0, :])
+        for q in range(4):
+            nc.scalar.dma_start(
+                xs[32 * q : 32 * q + 4, :].bitcast(I32), x_scales[0, 4 * q : 4 * q + 4, :].bitcast(I32)
+            )
+        nc.scalar.copy(warm2[:], warm[:])
+        nc.sync.dma_start(w_raw[:], w1.rearrange("(p j) m -> p j m", j=PACK))
+        for t in range(1, PACK):
+            nc.sync.dma_start(win[t][:], mem_rows[:, t, :])
+
+        xg = keep.tile([P, S], U32, name="xg", align_bytes=64)
+        xsg = keep.tile([P, S], U8, name="xsg", align_bytes=64)
+        old = [keep.tile([P, S], F32, name="old%d" % t, align_bytes=64) for t in range(PACK)]
+        new = [keep.tile([P, S], F32, name="new%d" % t, align_bytes=64) for t in range(PACK)]
+        wb = [keep.tile([P, 2 * P * PACK], BF16, name="wb%d" % h, align_bytes=64) for h in range(2)]
+        wq = [keep.tile([P, 2 * P], U32, name="wq%d" % h, align_bytes=64) for h in range(2)]
+        wsc = [keep.tile([P, 2 * P], U8, name="wsc%d" % h, align_bytes=64) for h in range(2)]
+        acc = [psum.tile([P, S], F32, name="acc%d" % t) for t in range(PACK)]
+        grouped = [keep.tile([P, CW * PACK], BF16, name="grouped%d" % c, align_bytes=64) for c in range(CHUNKS)]
+        codes = keep.tile([P, U], I32, name="codes", align_bytes=64)
+        scales = keep.tile([P, U], U8, name="scales", align_bytes=64)
+
+        w_view = w_raw[:].rearrange("p j (m t) -> p m j t", t=PACK)
+
+        def w_out(h):
+            return wb[h][:].rearrange("p (t m j) -> p m j t", t=2, j=PACK)
+
+        def gather_old(t):
+            nc.vector.tensor_copy(old[t][:], win[t][:].indirect(slot_t[:]))
+
+        def quant_w(h):
+            nc.vector.quantize_mx(out=wq[h][:].bitcast(FP8X4), scales=wsc[h][:], in_=wb[h][:])
+            for e in range(2):
+                cols = slice(e * P, (e + 1) * P)
+                nc.tensor.matmul_mx(
+                    out=acc[2 * h + e][:],
+                    lhsT=wq[h][:, cols].bitcast(FP8X4),
+                    lhsT_scale=wsc[h][:, cols],
+                    rhs=xg[:].bitcast(FP8X4),
+                    rhs_scale=xsg[:],
+                    start=True,
+                    stop=True,
+                )
+
+        def add(t):
+            nc.vector.tensor_tensor(new[t][:], old[t][:], acc[t][:], ADD)
+
+        def group_view(c):
+            return grouped[c][:].rearrange("p (c t) -> p c t", t=PACK)
+
+        def scatter(t):
+            nc.vector.tensor_copy(win[t][:].indirect(slot_t[:]), new[t][:])
+            nc.sync.dma_start(out_rows[:, t, :], win[t][:])
+
+        def round_plane(t, c, on_vector):
+            dst = group_view(c)[:, :, t]
+            src = win[t][:, c * CW : (c + 1) * CW]
+            if t == 2 and c < 2:
+                dst = group_view(c)[:, :, 2:4]
+                src = src.unsqueeze(2).to_broadcast([P, CW, 2])
+            if on_vector:
+                nc.vector.tensor_copy(dst, src)
+            else:
+                nc.scalar.copy(dst, src)
+
+        def quant_out(c):
+            cols = slice(c * CW, (c + 1) * CW)
+            nc.vector.quantize_mx(out=codes[:, cols].bitcast(FP8X4), scales=scales[:, cols], in_=grouped[c][:])
+
+        words_out = out_1[0].rearrange("p c r -> p (c r)").bitcast(I32)
+
+        nc.vector.tensor_copy(xg[:], xw[:].bitcast(U32).indirect(offs_t[:]))
+        gather_old(0)
+        nc.vector.tensor_copy(xsg[:], xs[:].indirect(offs_t[:]))
+        nc.vector.tensor_copy(w_out(0), w_view[:, :, :, 0:2])
+        nc.scalar.copy(w_out(1), w_view[:, :, :, 2:4])
+        quant_w(0)
+        gather_old(1)
+        add(0)
+        quant_w(1)
+        scatter(0)
+        for c in range(CHUNKS):
+            round_plane(0, c, False)
+        gather_old(2)
+        add(1)
+        gather_old(3)
+        scatter(1)
+        for c in range(CHUNKS):
+            round_plane(1, c, False)
+        add(2)
+        add(3)
+        scatter(2)
+        for c in range(CHUNKS):
+            round_plane(2, c, False)
+        scatter(3)
+        round_plane(3, 0, True)
+        round_plane(3, 2, False)
+        round_plane(3, 1, True)
+        round_plane(3, 3, False)
+        quant_out(0)
+        quant_out(1)
+        nc.sync.dma_start(words_out[:, 0 : 2 * CW], codes[:, 0 : 2 * CW])
+        quant_out(2)
+        nc.sync.dma_start(words_out[:, 2 * CW : 3 * CW], codes[:, 2 * CW : 3 * CW])
+        quant_out(3)
+        nc.scalar.dma_start(words_out[:, 3 * CW :], codes[:, 3 * CW :])
+        for q in range(4):
+            eng = nc.scalar if q == 3 else nc.sync
+            eng.dma_start(
+                out_2[0, 4 * q : 4 * q + 4, :].bitcast(I32), scales[32 * q : 32 * q + 4, :].bitcast(I32)
+            )

@@ -44,12 +44,12 @@ def tile_picked_idxput_add_po_kernel(
         nc.gpsimd.memset(warm[:], 0.0)
         nc.sync.dma_start(offs_t[:], offs)
         nc.sync.dma_start(xw[:], x_words[0].rearrange("p c r -> p (c r)").bitcast(I32))
-        nc.sync.dma_start(slot_t[:], slot)
-        nc.sync.dma_start(win[0][:], mem_rows[:, 0, :])
         for q in range(4):
-            nc.scalar.dma_start(
+            nc.sync.dma_start(
                 xs[32 * q : 32 * q + 4, :].bitcast(I32), x_scales[0, 4 * q : 4 * q + 4, :].bitcast(I32)
             )
+        nc.sync.dma_start(slot_t[:], slot)
+        nc.sync.dma_start(win[0][:], mem_rows[:, 0, :])
         nc.scalar.copy(warm2[:], warm[:])
         nc.sync.dma_start(w_raw[:], w1.rearrange("(p j) m -> p j m", j=PACK))
         for t in range(1, PACK):
@@ -59,6 +59,7 @@ def tile_picked_idxput_add_po_kernel(
         xsg = keep.tile([P, S], U8, name="xsg", align_bytes=64)
         old = [keep.tile([P, S], F32, name="old%d" % t, align_bytes=64) for t in range(PACK)]
         new = [keep.tile([P, S], F32, name="new%d" % t, align_bytes=64) for t in range(PACK)]
+        y = [keep.tile([P, S], F32, name="y%d" % t, align_bytes=64) for t in range(PACK)]
         wb = [keep.tile([P, 2 * P * PACK], BF16, name="wb%d" % h, align_bytes=64) for h in range(2)]
         wq = [keep.tile([P, 2 * P], U32, name="wq%d" % h, align_bytes=64) for h in range(2)]
         wsc = [keep.tile([P, 2 * P], U8, name="wsc%d" % h, align_bytes=64) for h in range(2)]
@@ -88,9 +89,10 @@ def tile_picked_idxput_add_po_kernel(
                     start=True,
                     stop=True,
                 )
+                nc.scalar.copy(y[2 * h + e][:], acc[2 * h + e][:])
 
         def add(t):
-            nc.vector.tensor_tensor(new[t][:], old[t][:], acc[t][:], ADD)
+            nc.gpsimd.tensor_tensor(new[t][:], old[t][:], y[t][:], ADD)
 
         def group_view(c):
             return grouped[c][:].rearrange("p (c t) -> p c t", t=PACK)
@@ -122,23 +124,18 @@ def tile_picked_idxput_add_po_kernel(
         nc.vector.tensor_copy(w_out(0), w_view[:, :, :, 0:2])
         nc.scalar.copy(w_out(1), w_view[:, :, :, 2:4])
         quant_w(0)
-        gather_old(1)
         add(0)
-        quant_w(1)
-        scatter(0)
-        for c in range(CHUNKS):
-            round_plane(0, c, False)
-        gather_old(2)
+        gather_old(1)
         add(1)
-        gather_old(3)
-        scatter(1)
-        for c in range(CHUNKS):
-            round_plane(1, c, False)
+        quant_w(1)
+        gather_old(2)
         add(2)
+        gather_old(3)
         add(3)
-        scatter(2)
-        for c in range(CHUNKS):
-            round_plane(2, c, False)
+        for t in range(PACK - 1):
+            scatter(t)
+            for c in range(CHUNKS):
+                round_plane(t, c, False)
         scatter(3)
         round_plane(3, 0, True)
         round_plane(3, 2, False)

@@ -63,8 +63,15 @@ def tile_picked_idxput_add_po_kernel(
         wb = [keep.tile([P, 2 * P * PACK], BF16, name="wb%d" % h, align_bytes=64) for h in range(2)]
         wq = [keep.tile([P, 2 * P], U32, name="wq%d" % h, align_bytes=64) for h in range(2)]
         wsc = [keep.tile([P, 2 * P], U8, name="wsc%d" % h, align_bytes=64) for h in range(2)]
-        acc = [psum.tile([P, S], F32, name="acc%d" % t) for t in range(PACK)]
-        grouped = [keep.tile([P, CW * PACK], BF16, name="grouped%d" % c, align_bytes=64) for c in range(CHUNKS)]
+        parts = [[slice(0, S // 2), slice(S // 2, S)]] + [[slice(0, S)]] * (PACK - 1)
+        acc = [
+            [psum.tile([P, part.stop - part.start], F32, name="acc%d_%d" % (t, part.start)) for part in parts[t]]
+            for t in range(PACK)
+        ]
+        spans = [slice(0, 2 * CW), slice(2 * CW, 3 * CW), slice(3 * CW, 4 * CW)]
+        grouped = [
+            keep.tile([P, (s.stop - s.start) * PACK], BF16, name="grouped%d" % s.start, align_bytes=64) for s in spans
+        ]
         codes = keep.tile([P, U], I32, name="codes", align_bytes=64)
         scales = keep.tile([P, U], U8, name="scales", align_bytes=64)
 
@@ -79,20 +86,23 @@ def tile_picked_idxput_add_po_kernel(
         def quant_w(h):
             nc.vector.quantize_mx(out=wq[h][:].bitcast(FP8X4), scales=wsc[h][:], in_=wb[h][:])
             for e in range(2):
+                t = 2 * h + e
                 cols = slice(e * P, (e + 1) * P)
-                nc.tensor.matmul_mx(
-                    out=acc[2 * h + e][:],
-                    lhsT=wq[h][:, cols].bitcast(FP8X4),
-                    lhsT_scale=wsc[h][:, cols],
-                    rhs=xg[:].bitcast(FP8X4),
-                    rhs_scale=xsg[:],
-                    start=True,
-                    stop=True,
-                )
-                nc.scalar.copy(y[2 * h + e][:], acc[2 * h + e][:])
+                for bank, part in zip(acc[t], parts[t]):
+                    nc.tensor.matmul_mx(
+                        out=bank[:],
+                        lhsT=wq[h][:, cols].bitcast(FP8X4),
+                        lhsT_scale=wsc[h][:, cols],
+                        rhs=xg[:, part].bitcast(FP8X4),
+                        rhs_scale=xsg[:, part],
+                        start=True,
+                        stop=True,
+                    )
+                    nc.scalar.copy(y[t][:, part], bank[:])
 
         def add(t):
-            nc.gpsimd.tensor_tensor(new[t][:], old[t][:], y[t][:], ADD)
+            for part in parts[t]:
+                nc.gpsimd.tensor_tensor(new[t][:, part], old[t][:, part], y[t][:, part], ADD)
 
         def group_view(c):
             return grouped[c][:].rearrange("p (c t) -> p c t", t=PACK)
@@ -101,20 +111,18 @@ def tile_picked_idxput_add_po_kernel(
             nc.vector.tensor_copy(win[t][:].indirect(slot_t[:]), new[t][:])
             nc.sync.dma_start(out_rows[:, t, :], win[t][:])
 
-        def round_plane(t, c, on_vector):
-            dst = group_view(c)[:, :, t]
-            src = win[t][:, c * CW : (c + 1) * CW]
-            if t == 2 and c < 2:
-                dst = group_view(c)[:, :, 2:4]
-                src = src.unsqueeze(2).to_broadcast([P, CW, 2])
-            if on_vector:
-                nc.vector.tensor_copy(dst, src)
-            else:
-                nc.scalar.copy(dst, src)
+        def round_plane(t, g):
+            dst = group_view(g)[:, :, t]
+            src = win[t][:, spans[g]]
+            if t == 2 and g == 0:
+                dst = group_view(g)[:, :, 2:4]
+                src = src.unsqueeze(2).to_broadcast([P, 2 * CW, 2])
+            nc.scalar.copy(dst, src)
 
         def quant_out(c):
             cols = slice(c * CW, (c + 1) * CW)
-            nc.vector.quantize_mx(out=codes[:, cols].bitcast(FP8X4), scales=scales[:, cols], in_=grouped[c][:])
+            src = grouped[0][:, c * CW * PACK : (c + 1) * CW * PACK] if c < 2 else grouped[c - 1][:]
+            nc.vector.quantize_mx(out=codes[:, cols].bitcast(FP8X4), scales=scales[:, cols], in_=src)
 
         words_out = out_1[0].rearrange("p c r -> p (c r)").bitcast(I32)
 
@@ -122,7 +130,8 @@ def tile_picked_idxput_add_po_kernel(
         gather_old(0)
         nc.vector.tensor_copy(xsg[:], xs[:].indirect(offs_t[:]))
         nc.vector.tensor_copy(w_out(0), w_view[:, :, :, 0:2])
-        nc.scalar.copy(w_out(1), w_view[:, :, :, 2:4])
+        nc.vector.tensor_copy(w_out(1)[:, 0:64], w_view[:, 0:64, :, 2:4])
+        nc.scalar.copy(w_out(1)[:, 64:128], w_view[:, 64:128, :, 2:4])
         quant_w(0)
         add(0)
         gather_old(1)
@@ -134,13 +143,14 @@ def tile_picked_idxput_add_po_kernel(
         add(3)
         for t in range(PACK - 1):
             scatter(t)
-            for c in range(CHUNKS):
-                round_plane(t, c, False)
+            for g in range(3):
+                round_plane(t, g)
         scatter(3)
-        round_plane(3, 0, True)
-        round_plane(3, 2, False)
-        round_plane(3, 1, True)
-        round_plane(3, 3, False)
+        round_plane(3, 1)
+        round_plane(3, 2)
+        for c in range(2):
+            cols = slice(c * CW, (c + 1) * CW)
+            nc.vector.tensor_copy(group_view(0)[:, cols, 3], win[3][:, cols])
         quant_out(0)
         quant_out(1)
         nc.sync.dma_start(words_out[:, 0 : 2 * CW], codes[:, 0 : 2 * CW])

@@ -58,16 +58,12 @@ def tile_picked_idxput_add_po_kernel(
         xg = keep.tile([P, S], U32, name="xg", align_bytes=64)
         xsg = keep.tile([P, S], U8, name="xsg", align_bytes=64)
         old = [keep.tile([P, S], F32, name="old%d" % t, align_bytes=64) for t in range(PACK)]
-        new = [keep.tile([P, S], F32, name="new%d" % t, align_bytes=64) for t in range(PACK)]
-        y = [keep.tile([P, S], F32, name="y%d" % t, align_bytes=64) for t in range(PACK)]
+        y = [keep.tile([P, 2, S], F32, name="y%d" % h, align_bytes=64) for h in range(2)]
         wb = [keep.tile([P, 2 * P * PACK], BF16, name="wb%d" % h, align_bytes=64) for h in range(2)]
         wq = [keep.tile([P, 2 * P], U32, name="wq%d" % h, align_bytes=64) for h in range(2)]
         wsc = [keep.tile([P, 2 * P], U8, name="wsc%d" % h, align_bytes=64) for h in range(2)]
-        parts = [[slice(0, S // 2), slice(S // 2, S)]] + [[slice(0, S)]] * (PACK - 1)
-        acc = [
-            [psum.tile([P, part.stop - part.start], F32, name="acc%d_%d" % (t, part.start)) for part in parts[t]]
-            for t in range(PACK)
-        ]
+        halves = [slice(0, S // 2), slice(S // 2, S)]
+        acc = [[psum.tile([P, 2, S // 2], F32, name="acc%d_%d" % (h, i)) for i in range(2)] for h in range(2)]
         spans = [slice(0, 2 * CW), slice(2 * CW, 3 * CW), slice(3 * CW, 4 * CW)]
         grouped = [
             keep.tile([P, (s.stop - s.start) * PACK], BF16, name="grouped%d" % s.start, align_bytes=64) for s in spans
@@ -85,12 +81,11 @@ def tile_picked_idxput_add_po_kernel(
 
         def quant_w(h):
             nc.vector.quantize_mx(out=wq[h][:].bitcast(FP8X4), scales=wsc[h][:], in_=wb[h][:])
-            for e in range(2):
-                t = 2 * h + e
-                cols = slice(e * P, (e + 1) * P)
-                for bank, part in zip(acc[t], parts[t]):
+            for bank, part in zip(acc[h], halves):
+                for e in range(2):
+                    cols = slice(e * P, (e + 1) * P)
                     nc.tensor.matmul_mx(
-                        out=bank[:],
+                        out=bank[:, e, :],
                         lhsT=wq[h][:, cols].bitcast(FP8X4),
                         lhsT_scale=wsc[h][:, cols],
                         rhs=xg[:, part].bitcast(FP8X4),
@@ -98,17 +93,13 @@ def tile_picked_idxput_add_po_kernel(
                         start=True,
                         stop=True,
                     )
-                    nc.scalar.copy(y[t][:, part], bank[:])
-
-        def add(t):
-            for part in parts[t]:
-                nc.gpsimd.tensor_tensor(new[t][:, part], old[t][:, part], y[t][:, part], ADD)
+                nc.scalar.copy(y[h][:, :, part], bank[:])
 
         def group_view(c):
             return grouped[c][:].rearrange("p (c t) -> p c t", t=PACK)
 
         def scatter(t):
-            nc.vector.tensor_copy(win[t][:].indirect(slot_t[:]), new[t][:])
+            nc.vector.tensor_tensor(win[t][:].indirect(slot_t[:]), old[t][:], y[t // 2][:, t % 2, :], ADD)
             nc.sync.dma_start(out_rows[:, t, :], win[t][:])
 
         def round_plane(t, g):
@@ -129,18 +120,14 @@ def tile_picked_idxput_add_po_kernel(
         nc.vector.tensor_copy(xg[:], xw[:].bitcast(U32).indirect(offs_t[:]))
         gather_old(0)
         nc.vector.tensor_copy(xsg[:], xs[:].indirect(offs_t[:]))
-        nc.vector.tensor_copy(w_out(0), w_view[:, :, :, 0:2])
-        nc.vector.tensor_copy(w_out(1)[:, 0:64], w_view[:, 0:64, :, 2:4])
-        nc.scalar.copy(w_out(1)[:, 64:128], w_view[:, 64:128, :, 2:4])
+        nc.scalar.copy(w_out(0)[:, 64:128], w_view[:, 64:128, :, 0:2])
+        nc.vector.tensor_copy(w_out(0)[:, 0:64], w_view[:, 0:64, :, 0:2])
+        nc.scalar.copy(w_out(1), w_view[:, :, :, 2:4])
         quant_w(0)
-        add(0)
         gather_old(1)
-        add(1)
         quant_w(1)
         gather_old(2)
-        add(2)
         gather_old(3)
-        add(3)
         for t in range(PACK - 1):
             scatter(t)
             for g in range(3):

@@ -16,8 +16,9 @@ ADD = mybir.AluOpType.add
 
 P = 128
 PACK = 4
-CHUNKS = 4
-CW = U // CHUNKS
+QUADRANTS = 4
+CHUNK = U // 4
+LAST = PACK - 1
 
 
 def tile_picked_idxput_add_po_kernel(
@@ -33,120 +34,120 @@ def tile_picked_idxput_add_po_kernel(
         xw = keep.tile([P, T], I32, name="xw", align_bytes=64)
         xs = keep.tile([P, T], U8, name="xs", align_bytes=64)
         w_raw = keep.tile([P, PACK, N], F32, name="w_raw", align_bytes=64)
-        win = [keep.tile([P, U], F32, name="win%d" % t, align_bytes=64) for t in range(PACK)]
-        warm = keep.tile([P, 8], F32, name="warm")
-        warm2 = keep.tile([P, 8], F32, name="warm2")
+        plane = [keep.tile([P, U], F32, name="plane%d" % t, align_bytes=64) for t in range(PACK)]
+        warm_out = keep.tile([P, 8], F32, name="warm_out")
 
         mem_rows = mem.rearrange("(p t) u -> p t u", t=PACK)
         out_rows = out_0.rearrange("(p t) u -> p t u", t=PACK)
 
         nc.vector.memset(xs[:].bitcast(I32), 0)
-        nc.gpsimd.memset(warm[:], 0.0)
+
         nc.sync.dma_start(offs_t[:], offs)
         nc.sync.dma_start(xw[:], x_words[0].rearrange("p c r -> p (c r)").bitcast(I32))
-        for q in range(4):
+        for q in range(QUADRANTS):
             nc.sync.dma_start(
                 xs[32 * q : 32 * q + 4, :].bitcast(I32), x_scales[0, 4 * q : 4 * q + 4, :].bitcast(I32)
             )
         nc.sync.dma_start(slot_t[:], slot)
-        nc.sync.dma_start(win[0][:], mem_rows[:, 0, :])
-        nc.scalar.copy(warm2[:], warm[:])
+        nc.sync.dma_start(plane[0][:], mem_rows[:, 0, :])
+        nc.scalar.copy(warm_out[:], plane[0][:, 0:8])
         nc.sync.dma_start(w_raw[:], w1.rearrange("(p j) m -> p j m", j=PACK))
         for t in range(1, PACK):
-            nc.sync.dma_start(win[t][:], mem_rows[:, t, :])
+            nc.sync.dma_start(plane[t][:], mem_rows[:, t, :])
 
-        xg = keep.tile([P, S], U32, name="xg", align_bytes=64)
-        xsg = keep.tile([P, S], U8, name="xsg", align_bytes=64)
+        xw_picked = keep.tile([P, S], U32, name="xw_picked", align_bytes=64)
+        xs_picked = keep.tile([P, S], U8, name="xs_picked", align_bytes=64)
         old = [keep.tile([P, S], F32, name="old%d" % t, align_bytes=64) for t in range(PACK)]
-        y = [keep.tile([P, 2, S], F32, name="y%d" % h, align_bytes=64) for h in range(2)]
-        wb = [keep.tile([P, 2 * P * PACK], BF16, name="wb%d" % h, align_bytes=64) for h in range(2)]
-        wq = [keep.tile([P, 2 * P], U32, name="wq%d" % h, align_bytes=64) for h in range(2)]
-        wsc = [keep.tile([P, 2 * P], U8, name="wsc%d" % h, align_bytes=64) for h in range(2)]
+        y = [keep.tile([P, 2, S], F32, name="y%d" % pair, align_bytes=64) for pair in range(2)]
+        w_bf = [keep.tile([P, 2 * P * PACK], BF16, name="w_bf%d" % pair, align_bytes=64) for pair in range(2)]
+        w_codes = [keep.tile([P, 2 * P], U32, name="w_codes%d" % pair, align_bytes=64) for pair in range(2)]
+        w_scales = [keep.tile([P, 2 * P], U8, name="w_scales%d" % pair, align_bytes=64) for pair in range(2)]
         halves = [slice(0, S // 2), slice(S // 2, S)]
-        acc = [[psum.tile([P, 2, S // 2], F32, name="acc%d_%d" % (h, i)) for i in range(2)] for h in range(2)]
-        spans = [slice(0, 2 * CW), slice(2 * CW, 3 * CW), slice(3 * CW, 4 * CW)]
+        acc = [[psum.tile([P, 2, S // 2], F32, name="acc%d_%d" % (pair, i)) for i in range(2)] for pair in range(2)]
+        spans = [slice(0, 2 * CHUNK), slice(2 * CHUNK, 3 * CHUNK), slice(3 * CHUNK, 4 * CHUNK)]
         grouped = [
             keep.tile([P, (s.stop - s.start) * PACK], BF16, name="grouped%d" % s.start, align_bytes=64) for s in spans
         ]
         codes = keep.tile([P, U], I32, name="codes", align_bytes=64)
         scales = keep.tile([P, U], U8, name="scales", align_bytes=64)
 
-        w_view = w_raw[:].rearrange("p j (m t) -> p m j t", t=PACK)
+        w_src = w_raw[:].rearrange("p j (m t) -> p m j t", t=PACK)
 
-        def w_out(h):
-            return wb[h][:].rearrange("p (t m j) -> p m j t", t=2, j=PACK)
+        def w_dst(pair):
+            return w_bf[pair][:].rearrange("p (t m j) -> p m j t", t=2, j=PACK)
 
         def gather_old(t):
-            nc.vector.tensor_copy(old[t][:], win[t][:].indirect(slot_t[:]))
+            nc.vector.tensor_copy(old[t][:], plane[t][:].indirect(slot_t[:]))
 
-        def quant_w(h):
-            nc.vector.quantize_mx(out=wq[h][:].bitcast(FP8X4), scales=wsc[h][:], in_=wb[h][:])
-            for bank, part in zip(acc[h], halves):
+        def project(pair):
+            nc.vector.quantize_mx(out=w_codes[pair][:].bitcast(FP8X4), scales=w_scales[pair][:], in_=w_bf[pair][:])
+            for bank, half in zip(acc[pair], halves):
                 for e in range(2):
                     cols = slice(e * P, (e + 1) * P)
                     nc.tensor.matmul_mx(
                         out=bank[:, e, :],
-                        lhsT=wq[h][:, cols].bitcast(FP8X4),
-                        lhsT_scale=wsc[h][:, cols],
-                        rhs=xg[:, part].bitcast(FP8X4),
-                        rhs_scale=xsg[:, part],
+                        lhsT=w_codes[pair][:, cols].bitcast(FP8X4),
+                        lhsT_scale=w_scales[pair][:, cols],
+                        rhs=xw_picked[:, half].bitcast(FP8X4),
+                        rhs_scale=xs_picked[:, half],
                         start=True,
                         stop=True,
                     )
-                nc.scalar.copy(y[h][:, :, part], bank[:])
+                nc.scalar.copy(y[pair][:, :, half], bank[:])
 
-        def group_view(c):
-            return grouped[c][:].rearrange("p (c t) -> p c t", t=PACK)
+        def by_plane(g):
+            return grouped[g][:].rearrange("p (c t) -> p c t", t=PACK)
 
-        def scatter(t):
-            nc.vector.tensor_tensor(win[t][:].indirect(slot_t[:]), old[t][:], y[t // 2][:, t % 2, :], ADD)
-            nc.sync.dma_start(out_rows[:, t, :], win[t][:])
+        def scatter_sums(t):
+            nc.vector.tensor_tensor(plane[t][:].indirect(slot_t[:]), old[t][:], y[t // 2][:, t % 2, :], ADD)
+            nc.sync.dma_start(out_rows[:, t, :], plane[t][:])
 
-        def round_plane(t, g):
-            dst = group_view(g)[:, :, t]
-            src = win[t][:, spans[g]]
-            if t == 2 and g == 0:
-                dst = group_view(g)[:, :, 2:4]
-                src = src.unsqueeze(2).to_broadcast([P, 2 * CW, 2])
+        def round_on_scalar(t, g):
+            dst = by_plane(g)[:, :, t]
+            src = plane[t][:, spans[g]]
+            if t == LAST - 1 and g == 0:
+                dst = by_plane(g)[:, :, LAST - 1 : PACK]
+                src = src.unsqueeze(2).to_broadcast([P, 2 * CHUNK, 2])
             nc.scalar.copy(dst, src)
 
-        def quant_out(c):
-            cols = slice(c * CW, (c + 1) * CW)
-            src = grouped[0][:, c * CW * PACK : (c + 1) * CW * PACK] if c < 2 else grouped[c - 1][:]
+        def quantise_result(c):
+            cols = slice(c * CHUNK, (c + 1) * CHUNK)
+            src = grouped[0][:, c * CHUNK * PACK : (c + 1) * CHUNK * PACK] if c < 2 else grouped[c - 1][:]
             nc.vector.quantize_mx(out=codes[:, cols].bitcast(FP8X4), scales=scales[:, cols], in_=src)
 
         words_out = out_1[0].rearrange("p c r -> p (c r)").bitcast(I32)
 
-        nc.vector.tensor_copy(xg[:], xw[:].bitcast(U32).indirect(offs_t[:]))
+        nc.vector.tensor_copy(xw_picked[:], xw[:].bitcast(U32).indirect(offs_t[:]))
         gather_old(0)
-        nc.vector.tensor_copy(xsg[:], xs[:].indirect(offs_t[:]))
-        nc.scalar.copy(w_out(0)[:, 64:128], w_view[:, 64:128, :, 0:2])
-        nc.vector.tensor_copy(w_out(0)[:, 0:64], w_view[:, 0:64, :, 0:2])
-        nc.scalar.copy(w_out(1), w_view[:, :, :, 2:4])
-        quant_w(0)
+        nc.vector.tensor_copy(xs_picked[:], xs[:].indirect(offs_t[:]))
+        nc.scalar.copy(w_dst(0)[:, P // 2 : P], w_src[:, P // 2 : P, :, 0:2])
+        nc.vector.tensor_copy(w_dst(0)[:, 0 : P // 2], w_src[:, 0 : P // 2, :, 0:2])
+        nc.scalar.copy(w_dst(1), w_src[:, :, :, 2:4])
+        project(0)
         gather_old(1)
-        quant_w(1)
+        project(1)
         gather_old(2)
         gather_old(3)
-        for t in range(PACK - 1):
-            scatter(t)
-            for g in range(3):
-                round_plane(t, g)
-        scatter(3)
-        round_plane(3, 1)
-        round_plane(3, 2)
+        for t in range(LAST):
+            scatter_sums(t)
+            for g in range(len(spans)):
+                round_on_scalar(t, g)
+
+        scatter_sums(LAST)
+        round_on_scalar(LAST, 1)
+        round_on_scalar(LAST, 2)
         for c in range(2):
-            cols = slice(c * CW, (c + 1) * CW)
-            nc.vector.tensor_copy(group_view(0)[:, cols, 3], win[3][:, cols])
-        quant_out(0)
-        quant_out(1)
-        nc.sync.dma_start(words_out[:, 0 : 2 * CW], codes[:, 0 : 2 * CW])
-        quant_out(2)
-        nc.sync.dma_start(words_out[:, 2 * CW : 3 * CW], codes[:, 2 * CW : 3 * CW])
-        quant_out(3)
-        nc.scalar.dma_start(words_out[:, 3 * CW :], codes[:, 3 * CW :])
-        for q in range(4):
-            eng = nc.scalar if q == 3 else nc.sync
-            eng.dma_start(
+            cols = slice(c * CHUNK, (c + 1) * CHUNK)
+            nc.vector.tensor_copy(by_plane(0)[:, cols, LAST], plane[LAST][:, cols])
+        quantise_result(0)
+        quantise_result(1)
+        nc.sync.dma_start(words_out[:, 0 : 2 * CHUNK], codes[:, 0 : 2 * CHUNK])
+        quantise_result(2)
+        nc.sync.dma_start(words_out[:, 2 * CHUNK : 3 * CHUNK], codes[:, 2 * CHUNK : 3 * CHUNK])
+        quantise_result(3)
+        nc.scalar.dma_start(words_out[:, 3 * CHUNK :], codes[:, 3 * CHUNK :])
+        for q in range(QUADRANTS):
+            queue = nc.scalar if q == QUADRANTS - 1 else nc.sync
+            queue.dma_start(
                 out_2[0, 4 * q : 4 * q + 4, :].bitcast(I32), scales[32 * q : 32 * q + 4, :].bitcast(I32)
             )

@@ -16,7 +16,7 @@ ADD = mybir.AluOpType.add
 
 P = 128
 PACK = 4
-QUADRANTS = 4
+SCALE_ROWS = 4
 CHUNK = U // 4
 LAST = PACK - 1
 
@@ -44,10 +44,8 @@ def tile_picked_idxput_add_po_kernel(
 
         nc.sync.dma_start(offs_t[:], offs)
         nc.sync.dma_start(xw[:], x_words[0].rearrange("p c r -> p (c r)").bitcast(I32))
-        for q in range(QUADRANTS):
-            nc.sync.dma_start(
-                xs[32 * q : 32 * q + 4, :].bitcast(I32), x_scales[0, 4 * q : 4 * q + 4, :].bitcast(I32)
-            )
+        for r in range(SCALE_ROWS):
+            nc.sync.dma_start(xs[r:P:32, :].bitcast(I32), x_scales[0, r : 16 : SCALE_ROWS, :].bitcast(I32))
         nc.sync.dma_start(slot_t[:], slot)
         nc.sync.dma_start(plane[0][:], mem_rows[:, 0, :])
         nc.scalar.copy(warm_out[:], plane[0][:, 0:8])
@@ -146,8 +144,6 @@ def tile_picked_idxput_add_po_kernel(
         nc.sync.dma_start(words_out[:, 2 * CHUNK : 3 * CHUNK], codes[:, 2 * CHUNK : 3 * CHUNK])
         quantise_result(3)
         nc.scalar.dma_start(words_out[:, 3 * CHUNK :], codes[:, 3 * CHUNK :])
-        for q in range(QUADRANTS):
-            queue = nc.scalar if q == QUADRANTS - 1 else nc.sync
-            queue.dma_start(
-                out_2[0, 4 * q : 4 * q + 4, :].bitcast(I32), scales[32 * q : 32 * q + 4, :].bitcast(I32)
-            )
+        for r in range(SCALE_ROWS):
+            queue = nc.scalar if r == SCALE_ROWS - 1 else nc.sync
+            queue.dma_start(out_2[0, r : 16 : SCALE_ROWS, :].bitcast(I32), scales[r:P:32, :].bitcast(I32))

@@ -19,6 +19,7 @@ PACK = 4
 SCALE_ROWS = 4
 CHUNK = U // 4
 LAST = PACK - 1
+W_ON_VECTOR = (64, 88)
 
 
 def tile_picked_idxput_add_po_kernel(
@@ -56,12 +57,14 @@ def tile_picked_idxput_add_po_kernel(
         xw_picked = keep.tile([P, S], U32, name="xw_picked", align_bytes=64)
         xs_picked = keep.tile([P, S], U8, name="xs_picked", align_bytes=64)
         old = [keep.tile([P, S], F32, name="old%d" % t, align_bytes=64) for t in range(PACK)]
-        y = [keep.tile([P, 2, S], F32, name="y%d" % pair, align_bytes=64) for pair in range(2)]
+        y_chain = keep.tile([P, 2 * S], F32, name="y_chain", align_bytes=64)
+        y = [y_chain[:, t * (S // 2) : t * (S // 2) + S] for t in range(LAST)] + [old[1][:]]
         w_bf = [keep.tile([P, 2 * P * PACK], BF16, name="w_bf%d" % pair, align_bytes=64) for pair in range(2)]
         w_codes = [keep.tile([P, 2 * P], U32, name="w_codes%d" % pair, align_bytes=64) for pair in range(2)]
         w_scales = [keep.tile([P, 2 * P], U8, name="w_scales%d" % pair, align_bytes=64) for pair in range(2)]
         halves = [slice(0, S // 2), slice(S // 2, S)]
-        acc = [[psum.tile([P, 2, S // 2], F32, name="acc%d_%d" % (pair, i)) for i in range(2)] for pair in range(2)]
+        acc_first = [psum.tile([P, S // 2], F32, name="acc_first%d" % i) for i in range(2)]
+        acc = [None] + [psum.tile([P, S], F32, name="acc%d" % t) for t in range(1, PACK)]
         spans = [slice(0, 2 * CHUNK), slice(2 * CHUNK, 3 * CHUNK), slice(3 * CHUNK, 4 * CHUNK)]
         grouped = [
             keep.tile([P, (s.stop - s.start) * PACK], BF16, name="grouped%d" % s.start, align_bytes=64) for s in spans
@@ -79,25 +82,30 @@ def tile_picked_idxput_add_po_kernel(
 
         def project(pair):
             nc.vector.quantize_mx(out=w_codes[pair][:].bitcast(FP8X4), scales=w_scales[pair][:], in_=w_bf[pair][:])
-            for bank, half in zip(acc[pair], halves):
-                for e in range(2):
-                    cols = slice(e * P, (e + 1) * P)
+            for e in range(2):
+                cols = slice(e * P, (e + 1) * P)
+                t = 2 * pair + e
+                pieces = zip(acc_first, halves) if t == 0 else [(acc[t], slice(0, S))]
+                for bank, entries in pieces:
                     nc.tensor.matmul_mx(
-                        out=bank[:, e, :],
+                        out=bank[:],
                         lhsT=w_codes[pair][:, cols].bitcast(FP8X4),
                         lhsT_scale=w_scales[pair][:, cols],
-                        rhs=xw_picked[:, half].bitcast(FP8X4),
-                        rhs_scale=xs_picked[:, half],
+                        rhs=xw_picked[:, entries].bitcast(FP8X4),
+                        rhs_scale=xs_picked[:, entries],
                         start=True,
                         stop=True,
                     )
-                nc.scalar.copy(y[pair][:, :, half], bank[:])
+                    if t == 0:
+                        nc.scalar.copy(y[t][:, entries], bank[:])
+                    elif t < LAST:
+                        nc.scalar.copy(y[t][:, halves[1]], bank[:, halves[1]])
 
         def by_plane(g):
             return grouped[g][:].rearrange("p (c t) -> p c t", t=PACK)
 
         def scatter_sums(t):
-            nc.vector.tensor_tensor(plane[t][:].indirect(slot_t[:]), old[t][:], y[t // 2][:, t % 2, :], ADD)
+            nc.vector.tensor_tensor(plane[t][:].indirect(slot_t[:]), old[t][:], y[t], ADD)
             nc.sync.dma_start(out_rows[:, t, :], plane[t][:])
 
         def round_on_scalar(t, g):
@@ -118,16 +126,20 @@ def tile_picked_idxput_add_po_kernel(
         nc.vector.tensor_copy(xw_picked[:], xw[:].bitcast(U32).indirect(offs_t[:]))
         gather_old(0)
         nc.vector.tensor_copy(xs_picked[:], xs[:].indirect(offs_t[:]))
-        nc.scalar.copy(w_dst(0)[:, P // 2 : P], w_src[:, P // 2 : P, :, 0:2])
-        nc.vector.tensor_copy(w_dst(0)[:, 0 : P // 2], w_src[:, 0 : P // 2, :, 0:2])
-        nc.scalar.copy(w_dst(1), w_src[:, :, :, 2:4])
+        for pair, cut in enumerate(W_ON_VECTOR):
+            planes = slice(2 * pair, 2 * pair + 2)
+            nc.vector.tensor_copy(w_dst(pair)[:, 0:cut], w_src[:, 0:cut, :, planes])
+            nc.scalar.copy(w_dst(pair)[:, cut:P], w_src[:, cut:P, :, planes])
         project(0)
-        gather_old(1)
         project(1)
-        gather_old(2)
-        gather_old(3)
+        gather_old(1)
         for t in range(LAST):
             scatter_sums(t)
+            if t + 1 < LAST:
+                nc.scalar.copy(y[t + 1][:, halves[0]], acc[t + 1][:, halves[0]])
+                gather_old(t + 2)
+            if t == 1:
+                nc.scalar.copy(y[LAST], acc[LAST][:])
             for g in range(len(spans)):
                 round_on_scalar(t, g)
 

@@ -36,6 +36,7 @@ def tile_picked_idxput_add_po_kernel(
         xs = keep.tile([P, T], U8, name="xs", align_bytes=64)
         w_raw = keep.tile([P, PACK, N], F32, name="w_raw", align_bytes=64)
         plane = [keep.tile([P, U], F32, name="plane%d" % t, align_bytes=64) for t in range(PACK)]
+        warm_in = keep.tile([P, 8], F32, name="warm_in")
         warm_out = keep.tile([P, 8], F32, name="warm_out")
 
         mem_rows = mem.rearrange("(p t) u -> p t u", t=PACK)
@@ -48,10 +49,10 @@ def tile_picked_idxput_add_po_kernel(
         for r in range(SCALE_ROWS):
             nc.sync.dma_start(xs[r:P:32, :].bitcast(I32), x_scales[0, r : 16 : SCALE_ROWS, :].bitcast(I32))
         nc.sync.dma_start(slot_t[:], slot)
-        nc.sync.dma_start(plane[0][:], mem_rows[:, 0, :])
-        nc.scalar.copy(warm_out[:], plane[0][:, 0:8])
+        nc.vector.memset(warm_in[:], 0.0)
+        nc.scalar.copy(warm_out[:], warm_in[:])
         nc.sync.dma_start(w_raw[:], w1.rearrange("(p j) m -> p j m", j=PACK))
-        for t in range(1, PACK):
+        for t in range(PACK):
             nc.sync.dma_start(plane[t][:], mem_rows[:, t, :])
 
         xw_picked = keep.tile([P, S], U32, name="xw_picked", align_bytes=64)
@@ -63,8 +64,8 @@ def tile_picked_idxput_add_po_kernel(
         w_codes = [keep.tile([P, 2 * P], U32, name="w_codes%d" % pair, align_bytes=64) for pair in range(2)]
         w_scales = [keep.tile([P, 2 * P], U8, name="w_scales%d" % pair, align_bytes=64) for pair in range(2)]
         halves = [slice(0, S // 2), slice(S // 2, S)]
-        acc_first = [psum.tile([P, S // 2], F32, name="acc_first%d" % i) for i in range(2)]
-        acc = [None] + [psum.tile([P, S], F32, name="acc%d" % t) for t in range(1, PACK)]
+        acc_first = [psum.tile([P, S // 2], F32, name="acc_first%d" % i, tag="first%d" % i) for i in range(2)]
+        acc = [None] + [psum.tile([P, S], F32, name="acc%d" % t) for t in range(1, LAST)]
         spans = [slice(0, 2 * CHUNK), slice(2 * CHUNK, 3 * CHUNK), slice(3 * CHUNK, 4 * CHUNK)]
         grouped = [
             keep.tile([P, (s.stop - s.start) * PACK], BF16, name="grouped%d" % s.start, align_bytes=64) for s in spans
@@ -80,11 +81,13 @@ def tile_picked_idxput_add_po_kernel(
         def gather_old(t):
             nc.vector.tensor_copy(old[t][:], plane[t][:].indirect(slot_t[:]))
 
-        def project(pair):
+        def quantise_w(pair):
             nc.vector.quantize_mx(out=w_codes[pair][:].bitcast(FP8X4), scales=w_scales[pair][:], in_=w_bf[pair][:])
-            for e in range(2):
+
+        def project(planes):
+            for t in planes:
+                pair, e = divmod(t, 2)
                 cols = slice(e * P, (e + 1) * P)
-                t = 2 * pair + e
                 pieces = zip(acc_first, halves) if t == 0 else [(acc[t], slice(0, S))]
                 for bank, entries in pieces:
                     nc.tensor.matmul_mx(
@@ -124,14 +127,18 @@ def tile_picked_idxput_add_po_kernel(
         words_out = out_1[0].rearrange("p c r -> p (c r)").bitcast(I32)
 
         nc.vector.tensor_copy(xw_picked[:], xw[:].bitcast(U32).indirect(offs_t[:]))
-        gather_old(0)
         nc.vector.tensor_copy(xs_picked[:], xs[:].indirect(offs_t[:]))
-        for pair, cut in enumerate(W_ON_VECTOR):
+        for pair, cut in zip((1, 0), W_ON_VECTOR):
             planes = slice(2 * pair, 2 * pair + 2)
             nc.vector.tensor_copy(w_dst(pair)[:, 0:cut], w_src[:, 0:cut, :, planes])
             nc.scalar.copy(w_dst(pair)[:, cut:P], w_src[:, cut:P, :, planes])
-        project(0)
-        project(1)
+        quantise_w(1)
+        project([2])
+        quantise_w(0)
+        project([0, 1])
+        acc.append(psum.tile([P, S], F32, name="acc3", tag="first0"))
+        project([3])
+        gather_old(0)
         gather_old(1)
         for t in range(LAST):
             scatter_sums(t)

@@ -20,6 +20,7 @@ SCALE_ROWS = 4
 CHUNK = U // 4
 LAST = PACK - 1
 W_ON_VECTOR = (64, 88)
+IN_WAIT = 96
 
 
 def tile_picked_idxput_add_po_kernel(
@@ -44,8 +45,8 @@ def tile_picked_idxput_add_po_kernel(
 
         nc.vector.memset(xs[:].bitcast(I32), 0)
 
-        nc.sync.dma_start(offs_t[:], offs)
         nc.sync.dma_start(xw[:], x_words[0].rearrange("p c r -> p (c r)").bitcast(I32))
+        nc.sync.dma_start(offs_t[:], offs)
         for r in range(SCALE_ROWS):
             nc.sync.dma_start(xs[r:P:32, :].bitcast(I32), x_scales[0, r : 16 : SCALE_ROWS, :].bitcast(I32))
         nc.sync.dma_start(slot_t[:], slot)
@@ -114,6 +115,8 @@ def tile_picked_idxput_add_po_kernel(
         def round_on_scalar(t, g):
             dst = by_plane(g)[:, :, t]
             src = plane[t][:, spans[g]]
+            if t == LAST - 1 and g == len(spans) - 1:
+                dst, src = dst[:, 0 : CHUNK - IN_WAIT], src[:, 0 : CHUNK - IN_WAIT]
             if t == LAST - 1 and g == 0:
                 dst = by_plane(g)[:, :, LAST - 1 : PACK]
                 src = src.unsqueeze(2).to_broadcast([P, 2 * CHUNK, 2])
@@ -151,6 +154,10 @@ def tile_picked_idxput_add_po_kernel(
                 round_on_scalar(t, g)
 
         scatter_sums(LAST)
+        nc.vector.tensor_copy(
+            by_plane(2)[:, CHUNK - IN_WAIT :, LAST - 1 : PACK],
+            plane[LAST - 1][:, U - IN_WAIT :].unsqueeze(2).to_broadcast([P, IN_WAIT, 2]),
+        )
         round_on_scalar(LAST, 1)
         round_on_scalar(LAST, 2)
         for c in range(2):

@@ -13,14 +13,14 @@ U16 = mybir.dt.uint16
 U8 = mybir.dt.uint8
 FP8X4 = mybir.dt.float8_e4m3fn_x4
 ADD = mybir.AluOpType.add
+COPY = mybir.ActivationFunctionType.Copy
 
 P = 128
 PACK = 4
 SCALE_ROWS = 4
+HALF = S // 2
 CHUNK = U // 4
-LAST = PACK - 1
-W_ON_VECTOR = (64, 88)
-IN_WAIT = 96
+W_ON_VECTOR = (84, 48)
 
 
 def tile_picked_idxput_add_po_kernel(
@@ -44,7 +44,6 @@ def tile_picked_idxput_add_po_kernel(
         out_rows = out_0.rearrange("(p t) u -> p t u", t=PACK)
 
         nc.vector.memset(xs[:].bitcast(I32), 0)
-
         nc.sync.dma_start(xw[:], x_words[0].rearrange("p c r -> p (c r)").bitcast(I32))
         nc.sync.dma_start(offs_t[:], offs)
         for r in range(SCALE_ROWS):
@@ -58,112 +57,143 @@ def tile_picked_idxput_add_po_kernel(
 
         xw_picked = keep.tile([P, S], U32, name="xw_picked", align_bytes=64)
         xs_picked = keep.tile([P, S], U8, name="xs_picked", align_bytes=64)
-        old = [keep.tile([P, S], F32, name="old%d" % t, align_bytes=64) for t in range(PACK)]
-        y_chain = keep.tile([P, 2 * S], F32, name="y_chain", align_bytes=64)
-        y = [y_chain[:, t * (S // 2) : t * (S // 2) + S] for t in range(LAST)] + [old[1][:]]
         w_bf = [keep.tile([P, 2 * P * PACK], BF16, name="w_bf%d" % pair, align_bytes=64) for pair in range(2)]
         w_codes = [keep.tile([P, 2 * P], U32, name="w_codes%d" % pair, align_bytes=64) for pair in range(2)]
         w_scales = [keep.tile([P, 2 * P], U8, name="w_scales%d" % pair, align_bytes=64) for pair in range(2)]
-        halves = [slice(0, S // 2), slice(S // 2, S)]
-        acc_first = [psum.tile([P, S // 2], F32, name="acc_first%d" % i, tag="first%d" % i) for i in range(2)]
-        acc = [None] + [psum.tile([P, S], F32, name="acc%d" % t) for t in range(1, LAST)]
-        spans = [slice(0, 2 * CHUNK), slice(2 * CHUNK, 3 * CHUNK), slice(3 * CHUNK, 4 * CHUNK)]
-        grouped = [
-            keep.tile([P, (s.stop - s.start) * PACK], BF16, name="grouped%d" % s.start, align_bytes=64) for s in spans
-        ]
+        halves = [slice(0, HALF), slice(HALF, S)]
+        slot_half = [slot_t[:, 0 : HALF // 16], slot_t[:, HALF // 16 : S // 16]]
+
+        old0 = keep.tile([P, S], F32, name="old0", align_bytes=64)
+        y0 = keep.tile([P, S], F32, name="y0", align_bytes=64)
+        acc0 = [psum.tile([P, HALF], F32, name="acc0_%d" % h) for h in range(2)]
+        row = [(3, 0, 128), (1, 0, 256), (2, 0, 512), (3, 128, 512), (1, 256, 512)]
+        old_first = keep.tile([P, S], F32, name="old_first", tag="first", align_bytes=64)
+        old_rest = keep.tile([P, 2 * S], F32, name="old_rest", tag="rest", align_bytes=64)
+        old = [old_first[:], old_rest[:, 0:S], old_rest[:, S : 2 * S]]
+        new = keep.tile([P, 3 * S], F32, name="new", align_bytes=64)
+        place = {}
+        at = 0
+        for t, lo, hi in row:
+            place[(t, lo)] = at
+            at = at + hi - lo
+
         codes = keep.tile([P, U], I32, name="codes", align_bytes=64)
         scales = keep.tile([P, U], U8, name="scales", align_bytes=64)
+        grouped = [keep.tile([P, CHUNK * PACK], BF16, name="grouped%d" % c, align_bytes=64) for c in range(4)]
 
         w_src = w_raw[:].rearrange("p j (m t) -> p m j t", t=PACK)
 
         def w_dst(pair):
             return w_bf[pair][:].rearrange("p (t m j) -> p m j t", t=2, j=PACK)
 
-        def gather_old(t):
-            nc.vector.tensor_copy(old[t][:], plane[t][:].indirect(slot_t[:]))
-
         def quantise_w(pair):
             nc.vector.quantize_mx(out=w_codes[pair][:].bitcast(FP8X4), scales=w_scales[pair][:], in_=w_bf[pair][:])
 
-        def project(planes):
-            for t in planes:
-                pair, e = divmod(t, 2)
-                cols = slice(e * P, (e + 1) * P)
-                pieces = zip(acc_first, halves) if t == 0 else [(acc[t], slice(0, S))]
-                for bank, entries in pieces:
-                    nc.tensor.matmul_mx(
-                        out=bank[:],
-                        lhsT=w_codes[pair][:, cols].bitcast(FP8X4),
-                        lhsT_scale=w_scales[pair][:, cols],
-                        rhs=xw_picked[:, entries].bitcast(FP8X4),
-                        rhs_scale=xs_picked[:, entries],
-                        start=True,
-                        stop=True,
-                    )
-                    if t == 0:
-                        nc.scalar.copy(y[t][:, entries], bank[:])
-                    elif t < LAST:
-                        nc.scalar.copy(y[t][:, halves[1]], bank[:, halves[1]])
+        def offsets(lo, hi):
+            return slot_t[:, lo // 16 : hi // 16]
 
-        def by_plane(g):
-            return grouped[g][:].rearrange("p (c t) -> p c t", t=PACK)
+        def project(out, t, lo, hi):
+            pair, e = divmod(t, 2)
+            cols = slice(e * P, (e + 1) * P)
+            nc.tensor.matmul_mx(
+                out=out,
+                lhsT=w_codes[pair][:, cols].bitcast(FP8X4),
+                lhsT_scale=w_scales[pair][:, cols],
+                rhs=xw_picked[:, lo:hi].bitcast(FP8X4),
+                rhs_scale=xs_picked[:, lo:hi],
+                start=True,
+                stop=True,
+            )
 
-        def scatter_sums(t):
-            nc.vector.tensor_tensor(plane[t][:].indirect(slot_t[:]), old[t][:], y[t], ADD)
-            nc.sync.dma_start(out_rows[:, t, :], plane[t][:])
+        def add_group(g, pieces):
+            bank = psum.tile([P, S], F32, name="acc_g%d" % g)
+            at = 0
+            for t, lo, hi in pieces:
+                project(bank[:, at : at + hi - lo], t, lo, hi)
+                at = at + hi - lo
+            nc.vector.tensor_tensor(new[:, g * S : (g + 1) * S], bank[:], old[g], ADD)
 
-        def round_on_scalar(t, g):
-            dst = by_plane(g)[:, :, t]
-            src = plane[t][:, spans[g]]
-            if t == LAST - 1 and g == len(spans) - 1:
-                dst, src = dst[:, 0 : CHUNK - IN_WAIT], src[:, 0 : CHUNK - IN_WAIT]
-            if t == LAST - 1 and g == 0:
-                dst = by_plane(g)[:, :, LAST - 1 : PACK]
-                src = src.unsqueeze(2).to_broadcast([P, 2 * CHUNK, 2])
-            nc.scalar.copy(dst, src)
+        def gather_on_scalar(t, lo, hi, at):
+            dst = old_first[:, at : at + hi - lo] if at < S else old_rest[:, at - S : at - S + hi - lo]
+            nc.scalar.activation(dst, plane[t][:].indirect(offsets(lo, hi)), COPY)
 
-        def quantise_result(c):
-            cols = slice(c * CHUNK, (c + 1) * CHUNK)
-            src = grouped[0][:, c * CHUNK * PACK : (c + 1) * CHUNK * PACK] if c < 2 else grouped[c - 1][:]
-            nc.vector.quantize_mx(out=codes[:, cols].bitcast(FP8X4), scales=scales[:, cols], in_=src)
-
-        words_out = out_1[0].rearrange("p c r -> p (c r)").bitcast(I32)
+        def scatter(t, lo, hi):
+            at = place[(t, lo)]
+            window = plane[t][:].indirect(offsets(lo, hi))
+            if t == 2:
+                nc.vector.tensor_copy(window, new[:, at : at + hi - lo])
+            else:
+                nc.scalar.activation(window, new[:, at : at + hi - lo], COPY)
+            if hi == S:
+                nc.sync.dma_start(out_rows[:, t, :], plane[t][:])
 
         nc.vector.tensor_copy(xw_picked[:], xw[:].bitcast(U32).indirect(offs_t[:]))
         nc.vector.tensor_copy(xs_picked[:], xs[:].indirect(offs_t[:]))
-        for pair, cut in zip((1, 0), W_ON_VECTOR):
+        for pair, cut in enumerate(W_ON_VECTOR):
             planes = slice(2 * pair, 2 * pair + 2)
             nc.vector.tensor_copy(w_dst(pair)[:, 0:cut], w_src[:, 0:cut, :, planes])
             nc.scalar.copy(w_dst(pair)[:, cut:P], w_src[:, cut:P, :, planes])
-        quantise_w(1)
-        project([2])
         quantise_w(0)
-        project([0, 1])
-        acc.append(psum.tile([P, S], F32, name="acc3", tag="first0"))
-        project([3])
-        gather_old(0)
-        gather_old(1)
-        for t in range(LAST):
-            scatter_sums(t)
-            if t + 1 < LAST:
-                nc.scalar.copy(y[t + 1][:, halves[0]], acc[t + 1][:, halves[0]])
-                gather_old(t + 2)
-            if t == 1:
-                nc.scalar.copy(y[LAST], acc[LAST][:])
-            for g in range(len(spans)):
-                round_on_scalar(t, g)
+        nc.vector.tensor_copy(old0[:, halves[0]], plane[0][:].indirect(slot_half[0]))
+        nc.scalar.activation(old0[:, halves[1]], plane[0][:].indirect(slot_half[1]), COPY)
+        quantise_w(1)
+        for h in range(2):
+            project(acc0[h][:], 0, h * HALF, (h + 1) * HALF)
+            nc.scalar.copy(y0[:, halves[h]], acc0[h][:])
+        nc.vector.tensor_tensor(plane[0][:].indirect(slot_t[:]), old0[:], y0[:], ADD)
+        nc.sync.dma_start(out_rows[:, 0, :], plane[0][:])
+        gather_on_scalar(1, 0, 256, 128)
+        gather_on_scalar(1, 256, 512, 1280)
+        gather_on_scalar(2, 0, 128, 384)
+        gather_on_scalar(2, 128, 512, 512)
+        gather_on_scalar(3, 0, 128, 0)
+        gather_on_scalar(3, 128, 512, 896)
+        add_group(0, [(3, 0, 128), (1, 0, 256), (2, 0, 128)])
+        add_group(1, [(2, 128, 384), (2, 384, 512), (3, 128, 256)])
+        add_group(2, [(3, 256, 512), (1, 256, 512)])
 
-        scatter_sums(LAST)
-        nc.vector.tensor_copy(
-            by_plane(2)[:, CHUNK - IN_WAIT :, LAST - 1 : PACK],
-            plane[LAST - 1][:, U - IN_WAIT :].unsqueeze(2).to_broadcast([P, IN_WAIT, 2]),
-        )
-        round_on_scalar(LAST, 1)
-        round_on_scalar(LAST, 2)
-        for c in range(2):
+        spans = [slice(0, CHUNK), slice(CHUNK, U)]
+        pairs = [
+            keep.tile([P, 2 * (s.stop - s.start) * 2], BF16, name="pairs%d" % i, tag=("first", "rest")[i], align_bytes=64)
+            for i, s in enumerate(spans)
+        ]
+
+        def round_plane(t):
+            pair, e = divmod(t, 2)
+            for i, s in enumerate(spans):
+                dst = pairs[i][:].rearrange("p (u c e) -> p u c e", u=2, e=2)[:, pair, :, e]
+                nc.vector.tensor_copy(dst, plane[t][:, s])
+
+        scatter(1, 0, 256)
+        scatter(3, 0, 128)
+        scatter(2, 0, 512)
+        scatter(1, 256, 512)
+        scatter(3, 128, 512)
+        round_plane(0)
+        round_plane(1)
+        round_plane(2)
+        round_plane(3)
+
+        def weave(c, on_scalar):
+            i, first = (0, 0) if c == 0 else (1, (c - 1) * CHUNK)
+            dt = U32 if on_scalar else I32
+            src = pairs[i][:].bitcast(dt).rearrange("p (u c) -> p c u", u=2)[:, first : first + CHUNK, :]
+            dst = grouped[c][:].bitcast(dt).rearrange("p (c u) -> p c u", u=2)
+            if on_scalar:
+                nc.scalar.copy(dst, src)
+            else:
+                nc.vector.tensor_copy(dst, src)
+
+        def quantise_result(c):
             cols = slice(c * CHUNK, (c + 1) * CHUNK)
-            nc.vector.tensor_copy(by_plane(0)[:, cols, LAST], plane[LAST][:, cols])
+            nc.vector.quantize_mx(out=codes[:, cols].bitcast(FP8X4), scales=scales[:, cols], in_=grouped[c][:])
+
+        words_out = out_1[0].rearrange("p c r -> p (c r)").bitcast(I32)
+        weave(0, True)
+        weave(1, True)
+        weave(3, True)
         quantise_result(0)
+        weave(2, False)
         quantise_result(1)
         nc.sync.dma_start(words_out[:, 0 : 2 * CHUNK], codes[:, 0 : 2 * CHUNK])
         quantise_result(2)

@@ -13,6 +13,7 @@ U16 = mybir.dt.uint16
 U8 = mybir.dt.uint8
 FP8X4 = mybir.dt.float8_e4m3fn_x4
 ADD = mybir.AluOpType.add
+MULT = mybir.AluOpType.mult
 COPY = mybir.ActivationFunctionType.Copy
 
 P = 128
@@ -21,6 +22,7 @@ SCALE_ROWS = 4
 HALF = S // 2
 CHUNK = U // 4
 W_ON_VECTOR = (84, 48)
+G3_ON_SCALAR = 384
 
 
 def tile_picked_idxput_add_po_kernel(
@@ -60,22 +62,25 @@ def tile_picked_idxput_add_po_kernel(
         w_bf = [keep.tile([P, 2 * P * PACK], BF16, name="w_bf%d" % pair, align_bytes=64) for pair in range(2)]
         w_codes = [keep.tile([P, 2 * P], U32, name="w_codes%d" % pair, align_bytes=64) for pair in range(2)]
         w_scales = [keep.tile([P, 2 * P], U8, name="w_scales%d" % pair, align_bytes=64) for pair in range(2)]
-        halves = [slice(0, HALF), slice(HALF, S)]
-        slot_half = [slot_t[:, 0 : HALF // 16], slot_t[:, HALF // 16 : S // 16]]
 
-        old0 = keep.tile([P, S], F32, name="old0", align_bytes=64)
-        y0 = keep.tile([P, S], F32, name="y0", align_bytes=64)
-        acc0 = [psum.tile([P, HALF], F32, name="acc0_%d" % h) for h in range(2)]
-        row = [(3, 0, 128), (1, 0, 256), (2, 0, 512), (3, 128, 512), (1, 256, 512)]
-        old_first = keep.tile([P, S], F32, name="old_first", tag="first", align_bytes=64)
-        old_rest = keep.tile([P, 2 * S], F32, name="old_rest", tag="rest", align_bytes=64)
-        old = [old_first[:], old_rest[:, 0:S], old_rest[:, S : 2 * S]]
-        new = keep.tile([P, 3 * S], F32, name="new", align_bytes=64)
+        old0 = keep.tile([P, HALF], F32, name="old0", align_bytes=64)
+        y0 = keep.tile([P, HALF], F32, name="y0", align_bytes=64)
+        acc0 = psum.tile([P, HALF], F32, name="acc0")
+        banks = [
+            [(2, 0, 128), (1, 0, 256), (0, 256, 384)],
+            [(0, 384, 512), (1, 256, 512), (2, 128, 256)],
+            [(2, 256, 512), (3, 0, 256)],
+            [(3, 256, 512)],
+        ]
         place = {}
         at = 0
-        for t, lo, hi in row:
-            place[(t, lo)] = at
-            at = at + hi - lo
+        for pieces in banks:
+            for t, lo, hi in pieces:
+                place[(t, lo)] = at
+                at = at + hi - lo
+        old = keep.tile([P, at], F32, name="old", align_bytes=64)
+        new = keep.tile([P, at], F32, name="new", align_bytes=64)
+        place[(3, G3_ON_SCALAR)] = place[(3, 0)] + G3_ON_SCALAR
 
         codes = keep.tile([P, U], I32, name="codes", align_bytes=64)
         scales = keep.tile([P, U], U8, name="scales", align_bytes=64)
@@ -105,22 +110,27 @@ def tile_picked_idxput_add_po_kernel(
                 stop=True,
             )
 
-        def add_group(g, pieces):
-            bank = psum.tile([P, S], F32, name="acc_g%d" % g)
-            at = 0
-            for t, lo, hi in pieces:
+        def add_group(g):
+            first = g * S
+            width = sum(hi - lo for t, lo, hi in banks[g])
+            bank = psum.tile([P, width], F32, name="acc_g%d" % g)
+            for t, lo, hi in banks[g]:
+                at = place[(t, lo)] - first
                 project(bank[:, at : at + hi - lo], t, lo, hi)
-                at = at + hi - lo
-            nc.vector.tensor_tensor(new[:, g * S : (g + 1) * S], bank[:], old[g], ADD)
+            nc.vector.tensor_tensor(new[:, first : first + width], bank[:], old[:, first : first + width], ADD)
 
-        def gather_on_scalar(t, lo, hi, at):
-            dst = old_first[:, at : at + hi - lo] if at < S else old_rest[:, at - S : at - S + hi - lo]
-            nc.scalar.activation(dst, plane[t][:].indirect(offsets(lo, hi)), COPY)
+        def gather(t, lo, hi, on_scalar=True):
+            at = place[(t, lo)]
+            window = plane[t][:].indirect(offsets(lo, hi))
+            if on_scalar:
+                nc.scalar.activation(old[:, at : at + hi - lo], window, COPY)
+            else:
+                nc.vector.tensor_copy(old[:, at : at + hi - lo], window)
 
         def scatter(t, lo, hi):
             at = place[(t, lo)]
             window = plane[t][:].indirect(offsets(lo, hi))
-            if t == 2:
+            if t % 2 == 0:
                 nc.vector.tensor_copy(window, new[:, at : at + hi - lo])
             else:
                 nc.scalar.activation(window, new[:, at : at + hi - lo], COPY)
@@ -134,27 +144,33 @@ def tile_picked_idxput_add_po_kernel(
             nc.vector.tensor_copy(w_dst(pair)[:, 0:cut], w_src[:, 0:cut, :, planes])
             nc.scalar.copy(w_dst(pair)[:, cut:P], w_src[:, cut:P, :, planes])
         quantise_w(0)
-        nc.vector.tensor_copy(old0[:, halves[0]], plane[0][:].indirect(slot_half[0]))
-        nc.scalar.activation(old0[:, halves[1]], plane[0][:].indirect(slot_half[1]), COPY)
+        nc.vector.tensor_copy(old0[:], plane[0][:].indirect(offsets(0, HALF)))
+        gather(0, 256, 512)
         quantise_w(1)
-        for h in range(2):
-            project(acc0[h][:], 0, h * HALF, (h + 1) * HALF)
-            nc.scalar.copy(y0[:, halves[h]], acc0[h][:])
-        nc.vector.tensor_tensor(plane[0][:].indirect(slot_t[:]), old0[:], y0[:], ADD)
-        nc.sync.dma_start(out_rows[:, 0, :], plane[0][:])
-        gather_on_scalar(1, 0, 256, 128)
-        gather_on_scalar(1, 256, 512, 1280)
-        gather_on_scalar(2, 0, 128, 384)
-        gather_on_scalar(2, 128, 512, 512)
-        gather_on_scalar(3, 0, 128, 0)
-        gather_on_scalar(3, 128, 512, 896)
-        add_group(0, [(3, 0, 128), (1, 0, 256), (2, 0, 128)])
-        add_group(1, [(2, 128, 384), (2, 384, 512), (3, 128, 256)])
-        add_group(2, [(3, 256, 512), (1, 256, 512)])
+        project(acc0[:], 0, 0, HALF)
+        nc.scalar.copy(y0[:], acc0[:])
+        nc.vector.tensor_tensor(plane[0][:].indirect(offsets(0, HALF)), old0[:], y0[:], ADD)
+        gather(1, 0, 256)
+        gather(1, 256, 512)
+        gather(2, 0, 128)
+        gather(2, 128, 512)
+        add_group(0)
+        add_group(1)
+        gather(3, 0, G3_ON_SCALAR)
+        gather(3, G3_ON_SCALAR, 512, on_scalar=False)
+        scatter(1, 0, 256)
+        scatter(2, 0, 128)
+        scatter(0, 256, 512)
+        add_group(2)
+        add_group(3)
+        scatter(1, 256, 512)
+        scatter(2, 128, 512)
+        scatter(3, 0, 256)
+        scatter(3, 256, 512)
 
         spans = [slice(0, CHUNK), slice(CHUNK, U)]
         pairs = [
-            keep.tile([P, 2 * (s.stop - s.start) * 2], BF16, name="pairs%d" % i, tag=("first", "rest")[i], align_bytes=64)
+            keep.tile([P, 2 * (s.stop - s.start) * 2], BF16, name="pairs%d" % i, align_bytes=64)
             for i, s in enumerate(spans)
         ]
 
@@ -162,17 +178,13 @@ def tile_picked_idxput_add_po_kernel(
             pair, e = divmod(t, 2)
             for i, s in enumerate(spans):
                 dst = pairs[i][:].rearrange("p (u c e) -> p u c e", u=2, e=2)[:, pair, :, e]
-                nc.vector.tensor_copy(dst, plane[t][:, s])
+                if pair == 0:
+                    nc.gpsimd.tensor_scalar(dst, plane[t][:, s], 1.0, 0.0, MULT, ADD)
+                else:
+                    nc.vector.tensor_copy(dst, plane[t][:, s])
 
-        scatter(1, 0, 256)
-        scatter(3, 0, 128)
-        scatter(2, 0, 512)
-        scatter(1, 256, 512)
-        scatter(3, 128, 512)
-        round_plane(0)
-        round_plane(1)
-        round_plane(2)
-        round_plane(3)
+        for t in range(PACK):
+            round_plane(t)
 
         def weave(c, on_scalar):
             i, first = (0, 0) if c == 0 else (1, (c - 1) * CHUNK)

@@ -21,7 +21,7 @@ PACK = 4
 SCALE_ROWS = 4
 HALF = S // 2
 CHUNK = U // 4
-W_ON_VECTOR = (84, 48)
+W_ON_VECTOR = (84, 72)
 G3_ON_SCALAR = 384
 
 
@@ -168,28 +168,23 @@ def tile_picked_idxput_add_po_kernel(
         scatter(3, 0, 256)
         scatter(3, 256, 512)
 
-        spans = [slice(0, CHUNK), slice(CHUNK, U)]
-        pairs = [
-            keep.tile([P, 2 * (s.stop - s.start) * 2], BF16, name="pairs%d" % i, align_bytes=64)
-            for i, s in enumerate(spans)
-        ]
+        pairs = keep.tile([P, 2 * U * 2], BF16, name="pairs", align_bytes=64)
+        by_pair = pairs[:].rearrange("p (u c e) -> p u c e", u=2, e=2)
+        chunks = [slice(c * CHUNK, (c + 1) * CHUNK) for c in range(4)]
 
-        def round_plane(t):
-            pair, e = divmod(t, 2)
-            for i, s in enumerate(spans):
-                dst = pairs[i][:].rearrange("p (u c e) -> p u c e", u=2, e=2)[:, pair, :, e]
-                if pair == 0:
-                    nc.gpsimd.tensor_scalar(dst, plane[t][:, s], 1.0, 0.0, MULT, ADD)
-                else:
-                    nc.vector.tensor_copy(dst, plane[t][:, s])
-
-        for t in range(PACK):
-            round_plane(t)
+        for t in range(2):
+            nc.gpsimd.tensor_scalar(by_pair[:, 0, :, t], plane[t][:], 1.0, 0.0, MULT, ADD)
+        nc.vector.tensor_copy(by_pair[:, 1, 0 : 3 * CHUNK, 0], plane[2][:, 0 : 3 * CHUNK])
+        nc.vector.tensor_copy(
+            by_pair[:, 1, chunks[3], :], plane[2][:, chunks[3]].unsqueeze(2).to_broadcast([P, CHUNK, 2])
+        )
+        for c in range(3):
+            nc.vector.tensor_copy(by_pair[:, 1, chunks[c], 1], plane[3][:, chunks[c]])
+        nc.scalar.copy(by_pair[:, 1, chunks[3], 1], plane[3][:, chunks[3]])
 
         def weave(c, on_scalar):
-            i, first = (0, 0) if c == 0 else (1, (c - 1) * CHUNK)
             dt = U32 if on_scalar else I32
-            src = pairs[i][:].bitcast(dt).rearrange("p (u c) -> p c u", u=2)[:, first : first + CHUNK, :]
+            src = pairs[:].bitcast(dt).rearrange("p (u c) -> p c u", u=2)[:, chunks[c], :]
             dst = grouped[c][:].bitcast(dt).rearrange("p (c u) -> p c u", u=2)
             if on_scalar:
                 nc.scalar.copy(dst, src)
@@ -201,11 +196,11 @@ def tile_picked_idxput_add_po_kernel(
             nc.vector.quantize_mx(out=codes[:, cols].bitcast(FP8X4), scales=scales[:, cols], in_=grouped[c][:])
 
         words_out = out_1[0].rearrange("p c r -> p (c r)").bitcast(I32)
-        weave(0, True)
-        weave(1, True)
+        weave(0, False)
+        weave(2, True)
         weave(3, True)
+        weave(1, False)
         quantise_result(0)
-        weave(2, False)
         quantise_result(1)
         nc.sync.dma_start(words_out[:, 0 : 2 * CHUNK], codes[:, 0 : 2 * CHUNK])
         quantise_result(2)

@@ -174,13 +174,13 @@ def tile_picked_idxput_add_po_kernel(
 
         for t in range(2):
             nc.gpsimd.tensor_scalar(by_pair[:, 0, :, t], plane[t][:], 1.0, 0.0, MULT, ADD)
-        nc.vector.tensor_copy(by_pair[:, 1, 0 : 3 * CHUNK, 0], plane[2][:, 0 : 3 * CHUNK])
+        nc.vector.tensor_copy(by_pair[:, 1, 0 : 2 * CHUNK, 0], plane[2][:, 0 : 2 * CHUNK])
         nc.vector.tensor_copy(
-            by_pair[:, 1, chunks[3], :], plane[2][:, chunks[3]].unsqueeze(2).to_broadcast([P, CHUNK, 2])
+            by_pair[:, 1, 2 * CHUNK : U, :], plane[2][:, 2 * CHUNK : U].unsqueeze(2).to_broadcast([P, 2 * CHUNK, 2])
         )
-        for c in range(3):
+        for c in range(2):
             nc.vector.tensor_copy(by_pair[:, 1, chunks[c], 1], plane[3][:, chunks[c]])
-        nc.scalar.copy(by_pair[:, 1, chunks[3], 1], plane[3][:, chunks[3]])
+            nc.scalar.copy(by_pair[:, 1, chunks[2 + c], 1], plane[3][:, chunks[2 + c]])
 
         def weave(c, on_scalar):
             dt = U32 if on_scalar else I32
@@ -201,10 +201,10 @@ def tile_picked_idxput_add_po_kernel(
         weave(3, True)
         weave(1, False)
         quantise_result(0)
+        nc.sync.dma_start(words_out[:, 0:CHUNK], codes[:, 0:CHUNK])
         quantise_result(1)
-        nc.sync.dma_start(words_out[:, 0 : 2 * CHUNK], codes[:, 0 : 2 * CHUNK])
         quantise_result(2)
-        nc.sync.dma_start(words_out[:, 2 * CHUNK : 3 * CHUNK], codes[:, 2 * CHUNK : 3 * CHUNK])
+        nc.sync.dma_start(words_out[:, CHUNK : 3 * CHUNK], codes[:, CHUNK : 3 * CHUNK])
         quantise_result(3)
         nc.scalar.dma_start(words_out[:, 3 * CHUNK :], codes[:, 3 * CHUNK :])
         for r in range(SCALE_ROWS):

@@ -22,7 +22,6 @@ SCALE_ROWS = 4
 HALF = S // 2
 CHUNK = U // 4
 W_ON_VECTOR = (84, 72)
-G3_ON_SCALAR = 384
 
 
 def tile_picked_idxput_add_po_kernel(
@@ -80,7 +79,6 @@ def tile_picked_idxput_add_po_kernel(
                 at = at + hi - lo
         old = keep.tile([P, at], F32, name="old", align_bytes=64)
         new = keep.tile([P, at], F32, name="new", align_bytes=64)
-        place[(3, G3_ON_SCALAR)] = place[(3, 0)] + G3_ON_SCALAR
 
         codes = keep.tile([P, U], I32, name="codes", align_bytes=64)
         scales = keep.tile([P, U], U8, name="scales", align_bytes=64)
@@ -119,13 +117,9 @@ def tile_picked_idxput_add_po_kernel(
                 project(bank[:, at : at + hi - lo], t, lo, hi)
             nc.vector.tensor_tensor(new[:, first : first + width], bank[:], old[:, first : first + width], ADD)
 
-        def gather(t, lo, hi, on_scalar=True):
+        def gather(t, lo, hi):
             at = place[(t, lo)]
-            window = plane[t][:].indirect(offsets(lo, hi))
-            if on_scalar:
-                nc.scalar.activation(old[:, at : at + hi - lo], window, COPY)
-            else:
-                nc.vector.tensor_copy(old[:, at : at + hi - lo], window)
+            nc.scalar.activation(old[:, at : at + hi - lo], plane[t][:].indirect(offsets(lo, hi)), COPY)
 
         def scatter(t, lo, hi):
             at = place[(t, lo)]
@@ -156,8 +150,7 @@ def tile_picked_idxput_add_po_kernel(
         gather(2, 128, 512)
         add_group(0)
         add_group(1)
-        gather(3, 0, G3_ON_SCALAR)
-        gather(3, G3_ON_SCALAR, 512, on_scalar=False)
+        gather(3, 0, 512)
         scatter(1, 0, 256)
         scatter(2, 0, 128)
         scatter(0, 256, 512)

@@ -66,8 +66,9 @@ def tile_picked_idxput_add_po_kernel(
         y0 = keep.tile([P, HALF], F32, name="y0", align_bytes=64)
         acc0 = psum.tile([P, HALF], F32, name="acc0")
         banks = [
-            [(2, 0, 128), (1, 0, 256), (0, 256, 384)],
-            [(0, 384, 512), (1, 256, 512), (2, 128, 256)],
+            [(2, 0, 128), (1, 0, 256)],
+            [(1, 256, 512)],
+            [(0, 256, 512), (2, 128, 256)],
             [(2, 256, 512), (3, 0, 256)],
             [(3, 256, 512)],
         ]
@@ -109,9 +110,9 @@ def tile_picked_idxput_add_po_kernel(
             )
 
         def add_group(g):
-            first = g * S
+            first = place[banks[g][0][:2]]
             width = sum(hi - lo for t, lo, hi in banks[g])
-            bank = psum.tile([P, width], F32, name="acc_g%d" % g)
+            bank = psum.tile([P, width], F32, name="acc_g%d" % g, tag="bank%d" % (0 if g == 1 else g))
             for t, lo, hi in banks[g]:
                 at = place[(t, lo)] - first
                 project(bank[:, at : at + hi - lo], t, lo, hi)
@@ -144,18 +145,18 @@ def tile_picked_idxput_add_po_kernel(
         project(acc0[:], 0, 0, HALF)
         nc.scalar.copy(y0[:], acc0[:])
         nc.vector.tensor_tensor(plane[0][:].indirect(offsets(0, HALF)), old0[:], y0[:], ADD)
-        gather(1, 0, 256)
-        gather(1, 256, 512)
+        gather(1, 0, 512)
         gather(2, 0, 128)
         gather(2, 128, 512)
         add_group(0)
-        add_group(1)
+        add_group(2)
         gather(3, 0, 512)
         scatter(1, 0, 256)
         scatter(2, 0, 128)
+        add_group(1)
         scatter(0, 256, 512)
-        add_group(2)
         add_group(3)
+        add_group(4)
         scatter(1, 256, 512)
         scatter(2, 128, 512)
         scatter(3, 0, 256)

@@ -65,19 +65,16 @@ def tile_picked_idxput_add_po_kernel(
         old0 = keep.tile([P, HALF], F32, name="old0", align_bytes=64)
         y0 = keep.tile([P, HALF], F32, name="y0", align_bytes=64)
         acc0 = psum.tile([P, HALF], F32, name="acc0")
-        banks = [
-            [(2, 0, 128), (1, 0, 256)],
-            [(1, 256, 512)],
-            [(0, 256, 512), (2, 128, 256)],
-            [(2, 256, 512), (3, 0, 256)],
-            [(3, 256, 512)],
+        row = [
+            (2, 0, 128), (1, 0, 256), (1, 256, 384), (1, 384, 512), (0, 256, 512),
+            (2, 128, 256), (2, 256, 384), (2, 384, 512), (3, 0, 256), (3, 256, 512),
         ]
+        banks = [row[0:2], row[3:6], [row[2], row[6]], row[7:9], row[9:10]]
         place = {}
         at = 0
-        for pieces in banks:
-            for t, lo, hi in pieces:
-                place[(t, lo)] = at
-                at = at + hi - lo
+        for t, lo, hi in row:
+            place[(t, lo)] = at
+            at = at + hi - lo
         old = keep.tile([P, at], F32, name="old", align_bytes=64)
         new = keep.tile([P, at], F32, name="new", align_bytes=64)
 
@@ -110,13 +107,23 @@ def tile_picked_idxput_add_po_kernel(
             )
 
         def add_group(g):
-            first = place[banks[g][0][:2]]
             width = sum(hi - lo for t, lo, hi in banks[g])
-            bank = psum.tile([P, width], F32, name="acc_g%d" % g, tag="bank%d" % (0 if g == 1 else g))
+            bank = psum.tile([P, width], F32, name="acc_g%d" % g)
+            at = 0
             for t, lo, hi in banks[g]:
-                at = place[(t, lo)] - first
                 project(bank[:, at : at + hi - lo], t, lo, hi)
-            nc.vector.tensor_tensor(new[:, first : first + width], bank[:], old[:, first : first + width], ADD)
+                at = at + hi - lo
+            first, last = place[banks[g][0][:2]], place[banks[g][-1][:2]]
+            if last - first < width:
+                cols = slice(first, first + width)
+                nc.vector.tensor_tensor(new[:, cols], bank[:], old[:, cols], ADD)
+            else:
+                step = last - first
+                dst, src = (
+                    x[:, first : first + 2 * step].rearrange("p (s c) -> p s c", s=2)[:, :, 0 : width // 2]
+                    for x in (new, old)
+                )
+                nc.vector.tensor_tensor(dst, bank[:].rearrange("p (s c) -> p s c", s=2), src, ADD)
 
         def gather(t, lo, hi):
             at = place[(t, lo)]
@@ -149,12 +156,12 @@ def tile_picked_idxput_add_po_kernel(
         gather(2, 0, 128)
         gather(2, 128, 512)
         add_group(0)
+        add_group(1)
         add_group(2)
         gather(3, 0, 512)
         scatter(1, 0, 256)
-        scatter(2, 0, 128)
-        add_group(1)
         scatter(0, 256, 512)
+        scatter(2, 0, 128)
         add_group(3)
         add_group(4)
         scatter(1, 256, 512)

@@ -19,9 +19,10 @@ COPY = mybir.ActivationFunctionType.Copy
 P = 128
 PACK = 4
 SCALE_ROWS = 4
+QUAD = 32
 HALF = S // 2
 CHUNK = U // 4
-W_ON_VECTOR = (84, 72)
+W_ON_VECTOR = 88
 
 
 def tile_picked_idxput_add_po_kernel(
@@ -35,6 +36,7 @@ def tile_picked_idxput_add_po_kernel(
         offs_t = keep.tile([P, S // 16], U16, name="offs_t")
         slot_t = keep.tile([P, S // 16], U16, name="slot_t")
         xw = keep.tile([P, T], I32, name="xw", align_bytes=64)
+        xs_stage = keep.tile([P, 2 * T], U8, name="xs_stage", align_bytes=64)
         xs = keep.tile([P, T], U8, name="xs", align_bytes=64)
         w_raw = keep.tile([P, PACK, N], F32, name="w_raw", align_bytes=64)
         plane = [keep.tile([P, U], F32, name="plane%d" % t, align_bytes=64) for t in range(PACK)]
@@ -44,39 +46,38 @@ def tile_picked_idxput_add_po_kernel(
         mem_rows = mem.rearrange("(p t) u -> p t u", t=PACK)
         out_rows = out_0.rearrange("(p t) u -> p t u", t=PACK)
 
-        nc.vector.memset(xs[:].bitcast(I32), 0)
-        nc.sync.dma_start(xw[:], x_words[0].rearrange("p c r -> p (c r)").bitcast(I32))
+        def load_scale_rows(queue, h):
+            rows = x_scales[0, 8 * h : 8 * h + 8, :].bitcast(I32).rearrange("(q r) c -> r q c", q=2)
+            stage = xs_stage[64 * h : 64 * h + SCALE_ROWS, :].bitcast(I32)
+            queue.dma_start(stage.rearrange("r (q c) -> r q c", q=2), rows)
+
+        load_scale_rows(nc.sync, 0)
+        load_scale_rows(nc.scalar, 1)
         nc.sync.dma_start(offs_t[:], offs)
-        for r in range(SCALE_ROWS):
-            nc.sync.dma_start(xs[r:P:32, :].bitcast(I32), x_scales[0, r : 16 : SCALE_ROWS, :].bitcast(I32))
-        nc.sync.dma_start(slot_t[:], slot)
-        nc.vector.memset(warm_in[:], 0.0)
-        nc.scalar.copy(warm_out[:], warm_in[:])
         nc.sync.dma_start(w_raw[:], w1.rearrange("(p j) m -> p j m", j=PACK))
+        nc.sync.dma_start(xw[:], x_words[0].rearrange("p c r -> p (c r)").bitcast(I32))
+        nc.sync.dma_start(slot_t[:], slot)
         for t in range(PACK):
             nc.sync.dma_start(plane[t][:], mem_rows[:, t, :])
+        nc.vector.memset(xs[:].bitcast(I32), 0)
+        nc.vector.memset(warm_in[:], 0.0)
+        nc.scalar.copy(warm_out[:], warm_in[:])
 
-        xw_picked = keep.tile([P, S], U32, name="xw_picked", align_bytes=64)
+        for q in range(4):
+            h, e = divmod(q, 2)
+            nc.vector.tensor_copy(
+                xs[QUAD * q : QUAD * q + SCALE_ROWS, :].bitcast(I32),
+                xs_stage[64 * h : 64 * h + SCALE_ROWS, e * T : (e + 1) * T].bitcast(I32),
+            )
+
+        xw_picked = [keep.tile([P, HALF], U32, name="xw_picked%d" % h, align_bytes=64) for h in range(2)]
         xs_picked = keep.tile([P, S], U8, name="xs_picked", align_bytes=64)
         w_bf = [keep.tile([P, 2 * P * PACK], BF16, name="w_bf%d" % pair, align_bytes=64) for pair in range(2)]
         w_codes = [keep.tile([P, 2 * P], U32, name="w_codes%d" % pair, align_bytes=64) for pair in range(2)]
         w_scales = [keep.tile([P, 2 * P], U8, name="w_scales%d" % pair, align_bytes=64) for pair in range(2)]
 
-        old0 = keep.tile([P, HALF], F32, name="old0", align_bytes=64)
-        y0 = keep.tile([P, HALF], F32, name="y0", align_bytes=64)
-        acc0 = psum.tile([P, HALF], F32, name="acc0")
-        row = [
-            (2, 0, 128), (1, 0, 256), (1, 256, 384), (1, 384, 512), (0, 256, 512),
-            (2, 128, 256), (2, 256, 384), (2, 384, 512), (3, 0, 256), (3, 256, 512),
-        ]
-        banks = [row[0:2], row[3:6], [row[2], row[6]], row[7:9], row[9:10]]
-        place = {}
-        at = 0
-        for t, lo, hi in row:
-            place[(t, lo)] = at
-            at = at + hi - lo
-        old = keep.tile([P, at], F32, name="old", align_bytes=64)
-        new = keep.tile([P, at], F32, name="new", align_bytes=64)
+        old = keep.tile([P, PACK * S], F32, name="old", align_bytes=64)
+        new = keep.tile([P, PACK * S], F32, name="new", align_bytes=64)
 
         codes = keep.tile([P, U], I32, name="codes", align_bytes=64)
         scales = keep.tile([P, U], U8, name="scales", align_bytes=64)
@@ -96,78 +97,98 @@ def tile_picked_idxput_add_po_kernel(
         def project(out, t, lo, hi):
             pair, e = divmod(t, 2)
             cols = slice(e * P, (e + 1) * P)
+            h = lo // HALF
             nc.tensor.matmul_mx(
                 out=out,
                 lhsT=w_codes[pair][:, cols].bitcast(FP8X4),
                 lhsT_scale=w_scales[pair][:, cols],
-                rhs=xw_picked[:, lo:hi].bitcast(FP8X4),
+                rhs=xw_picked[h][:, lo - h * HALF : hi - h * HALF].bitcast(FP8X4),
                 rhs_scale=xs_picked[:, lo:hi],
                 start=True,
                 stop=True,
             )
 
-        def add_group(g):
-            width = sum(hi - lo for t, lo, hi in banks[g])
-            bank = psum.tile([P, width], F32, name="acc_g%d" % g)
+        def add(name, pieces):
+            width = sum(hi - lo for t, lo, hi in pieces)
+            bank = psum.tile([P, width], F32, name=name)
             at = 0
-            for t, lo, hi in banks[g]:
+            for t, lo, hi in pieces:
                 project(bank[:, at : at + hi - lo], t, lo, hi)
                 at = at + hi - lo
-            first, last = place[banks[g][0][:2]], place[banks[g][-1][:2]]
-            if last - first < width:
+            first, last = (t * S + lo for t, lo, hi in (pieces[0], pieces[min(1, len(pieces) - 1)]))
+            step = last - first
+            if step < width:
                 cols = slice(first, first + width)
                 nc.vector.tensor_tensor(new[:, cols], bank[:], old[:, cols], ADD)
+                return
+            if width == 2 * P:
+                dst, src = (
+                    x[:].rearrange("p (b c) -> p b c", c=P)[:, first // P : last // P + 1 : step // P, :]
+                    for x in (new, old)
+                )
             else:
-                step = last - first
                 dst, src = (
                     x[:, first : first + 2 * step].rearrange("p (s c) -> p s c", s=2)[:, :, 0 : width // 2]
                     for x in (new, old)
                 )
-                nc.vector.tensor_tensor(dst, bank[:].rearrange("p (s c) -> p s c", s=2), src, ADD)
+            nc.vector.tensor_tensor(dst, bank[:].rearrange("p (s c) -> p s c", s=2), src, ADD)
 
-        def gather(t, lo, hi):
-            at = place[(t, lo)]
-            nc.scalar.activation(old[:, at : at + hi - lo], plane[t][:].indirect(offsets(lo, hi)), COPY)
+        def gather(t, lo, hi, on_vector=False):
+            dst = old[:, t * S + lo : t * S + hi]
+            if on_vector:
+                nc.vector.tensor_copy(dst, plane[t][:].indirect(offsets(lo, hi)))
+            else:
+                nc.scalar.activation(dst, plane[t][:].indirect(offsets(lo, hi)), COPY)
 
         def scatter(t, lo, hi):
-            at = place[(t, lo)]
+            src = new[:, t * S + lo : t * S + hi]
             window = plane[t][:].indirect(offsets(lo, hi))
             if t % 2 == 0:
-                nc.vector.tensor_copy(window, new[:, at : at + hi - lo])
+                nc.vector.tensor_copy(window, src)
             else:
-                nc.scalar.activation(window, new[:, at : at + hi - lo], COPY)
-            if hi == S:
-                nc.sync.dma_start(out_rows[:, t, :], plane[t][:])
+                nc.scalar.activation(window, src, COPY)
 
-        nc.vector.tensor_copy(xw_picked[:], xw[:].bitcast(U32).indirect(offs_t[:]))
+        def store(t):
+            nc.sync.dma_start(out_rows[:, t, :], plane[t][:])
+
         nc.vector.tensor_copy(xs_picked[:], xs[:].indirect(offs_t[:]))
-        for pair, cut in enumerate(W_ON_VECTOR):
-            planes = slice(2 * pair, 2 * pair + 2)
-            nc.vector.tensor_copy(w_dst(pair)[:, 0:cut], w_src[:, 0:cut, :, planes])
-            nc.scalar.copy(w_dst(pair)[:, cut:P], w_src[:, cut:P, :, planes])
+        nc.vector.tensor_copy(w_dst(0)[:, 0:W_ON_VECTOR], w_src[:, 0:W_ON_VECTOR, :, 0:2])
+        nc.scalar.copy(w_dst(0)[:, W_ON_VECTOR:P], w_src[:, W_ON_VECTOR:P, :, 0:2])
+        nc.scalar.copy(w_dst(1), w_src[:, :, :, 2:4])
         quantise_w(0)
-        nc.vector.tensor_copy(old0[:], plane[0][:].indirect(offsets(0, HALF)))
-        gather(0, 256, 512)
+        for h in range(2):
+            nc.vector.tensor_copy(
+                xw_picked[h][:], xw[:].bitcast(U32).indirect(offs_t[:, h * HALF // 16 : (h + 1) * HALF // 16])
+            )
         quantise_w(1)
-        project(acc0[:], 0, 0, HALF)
-        nc.scalar.copy(y0[:], acc0[:])
-        nc.vector.tensor_tensor(plane[0][:].indirect(offsets(0, HALF)), old0[:], y0[:], ADD)
+        gather(0, 0, 256)
+        gather(0, 256, 384)
+        gather(0, 384, 512, True)
+        add("acc_a", [(0, 0, 256)])
+        add("acc_b", [(0, 384, 512)])
+        scatter(0, 0, 256)
         gather(1, 0, 512)
-        gather(2, 0, 128)
-        gather(2, 128, 512)
-        add_group(0)
-        add_group(1)
-        add_group(2)
-        gather(3, 0, 512)
-        scatter(1, 0, 256)
-        scatter(0, 256, 512)
-        scatter(2, 0, 128)
-        add_group(3)
-        add_group(4)
+        gather(2, 0, 384)
+        gather(2, 384, 512)
+        add("acc_z", [(1, 0, 256)])
+        add("acc_x", [(1, 256, 512), (2, 0, 128)])
+        add("acc_y", [(2, 128, 256), (2, 256, 384)])
+        gather(3, 0, 128)
+        gather(3, 128, 384)
+        gather(3, 384, 512, True)
+        add("acc_d", [(0, 256, 384), (3, 0, 128)])
         scatter(1, 256, 512)
-        scatter(2, 128, 512)
-        scatter(3, 0, 256)
-        scatter(3, 256, 512)
+        scatter(0, 256, 512)
+        store(0)
+        scatter(3, 0, 128)
+        add("acc_r", [(2, 384, 512), (3, 128, 256)])
+        add("acc_w", [(3, 256, 512)])
+        scatter(1, 0, 256)
+        store(1)
+        scatter(2, 0, 512)
+        store(2)
+        scatter(3, 128, 512)
+        store(3)
 
         pairs = keep.tile([P, 2 * U * 2], BF16, name="pairs", align_bytes=64)
         by_pair = pairs[:].rearrange("p (u c e) -> p u c e", u=2, e=2)
@@ -175,10 +196,10 @@ def tile_picked_idxput_add_po_kernel(
 
         for t in range(2):
             nc.gpsimd.tensor_scalar(by_pair[:, 0, :, t], plane[t][:], 1.0, 0.0, MULT, ADD)
-        nc.vector.tensor_copy(by_pair[:, 1, 0 : 2 * CHUNK, 0], plane[2][:, 0 : 2 * CHUNK])
         nc.vector.tensor_copy(
             by_pair[:, 1, 2 * CHUNK : U, :], plane[2][:, 2 * CHUNK : U].unsqueeze(2).to_broadcast([P, 2 * CHUNK, 2])
         )
+        nc.vector.tensor_copy(by_pair[:, 1, 0 : 2 * CHUNK, 0], plane[2][:, 0 : 2 * CHUNK])
         for c in range(2):
             nc.vector.tensor_copy(by_pair[:, 1, chunks[c], 1], plane[3][:, chunks[c]])
             nc.scalar.copy(by_pair[:, 1, chunks[2 + c], 1], plane[3][:, chunks[2 + c]])

@@ -19,10 +19,8 @@ COPY = mybir.ActivationFunctionType.Copy
 P = 128
 PACK = 4
 SCALE_ROWS = 4
-QUAD = 32
-HALF = S // 2
 CHUNK = U // 4
-W_ON_VECTOR = 88
+W_ON_VECTOR = (84, 72)
 
 
 def tile_picked_idxput_add_po_kernel(
@@ -36,7 +34,6 @@ def tile_picked_idxput_add_po_kernel(
         offs_t = keep.tile([P, S // 16], U16, name="offs_t")
         slot_t = keep.tile([P, S // 16], U16, name="slot_t")
         xw = keep.tile([P, T], I32, name="xw", align_bytes=64)
-        xs_stage = keep.tile([P, 2 * T], U8, name="xs_stage", align_bytes=64)
         xs = keep.tile([P, T], U8, name="xs", align_bytes=64)
         w_raw = keep.tile([P, PACK, N], F32, name="w_raw", align_bytes=64)
         plane = [keep.tile([P, U], F32, name="plane%d" % t, align_bytes=64) for t in range(PACK)]
@@ -46,31 +43,19 @@ def tile_picked_idxput_add_po_kernel(
         mem_rows = mem.rearrange("(p t) u -> p t u", t=PACK)
         out_rows = out_0.rearrange("(p t) u -> p t u", t=PACK)
 
-        def load_scale_rows(queue, h):
-            rows = x_scales[0, 8 * h : 8 * h + 8, :].bitcast(I32).rearrange("(q r) c -> r q c", q=2)
-            stage = xs_stage[64 * h : 64 * h + SCALE_ROWS, :].bitcast(I32)
-            queue.dma_start(stage.rearrange("r (q c) -> r q c", q=2), rows)
-
-        load_scale_rows(nc.sync, 0)
-        load_scale_rows(nc.scalar, 1)
-        nc.sync.dma_start(offs_t[:], offs)
-        nc.sync.dma_start(w_raw[:], w1.rearrange("(p j) m -> p j m", j=PACK))
-        nc.sync.dma_start(xw[:], x_words[0].rearrange("p c r -> p (c r)").bitcast(I32))
-        nc.sync.dma_start(slot_t[:], slot)
-        for t in range(PACK):
-            nc.sync.dma_start(plane[t][:], mem_rows[:, t, :])
         nc.vector.memset(xs[:].bitcast(I32), 0)
+        nc.sync.dma_start(xw[:], x_words[0].rearrange("p c r -> p (c r)").bitcast(I32))
+        nc.sync.dma_start(offs_t[:], offs)
+        for r in range(SCALE_ROWS):
+            nc.sync.dma_start(xs[r:P:32, :].bitcast(I32), x_scales[0, r : 16 : SCALE_ROWS, :].bitcast(I32))
+        nc.sync.dma_start(slot_t[:], slot)
         nc.vector.memset(warm_in[:], 0.0)
         nc.scalar.copy(warm_out[:], warm_in[:])
+        nc.sync.dma_start(w_raw[:], w1.rearrange("(p j) m -> p j m", j=PACK))
+        for t in range(PACK):
+            nc.sync.dma_start(plane[t][:], mem_rows[:, t, :])
 
-        for q in range(4):
-            h, e = divmod(q, 2)
-            nc.vector.tensor_copy(
-                xs[QUAD * q : QUAD * q + SCALE_ROWS, :].bitcast(I32),
-                xs_stage[64 * h : 64 * h + SCALE_ROWS, e * T : (e + 1) * T].bitcast(I32),
-            )
-
-        xw_picked = [keep.tile([P, HALF], U32, name="xw_picked%d" % h, align_bytes=64) for h in range(2)]
+        xw_picked = keep.tile([P, S], U32, name="xw_picked", align_bytes=64)
         xs_picked = keep.tile([P, S], U8, name="xs_picked", align_bytes=64)
         w_bf = [keep.tile([P, 2 * P * PACK], BF16, name="w_bf%d" % pair, align_bytes=64) for pair in range(2)]
         w_codes = [keep.tile([P, 2 * P], U32, name="w_codes%d" % pair, align_bytes=64) for pair in range(2)]
@@ -97,12 +82,11 @@ def tile_picked_idxput_add_po_kernel(
         def project(out, t, lo, hi):
             pair, e = divmod(t, 2)
             cols = slice(e * P, (e + 1) * P)
-            h = lo // HALF
             nc.tensor.matmul_mx(
                 out=out,
                 lhsT=w_codes[pair][:, cols].bitcast(FP8X4),
                 lhsT_scale=w_scales[pair][:, cols],
-                rhs=xw_picked[h][:, lo - h * HALF : hi - h * HALF].bitcast(FP8X4),
+                rhs=xw_picked[:, lo:hi].bitcast(FP8X4),
                 rhs_scale=xs_picked[:, lo:hi],
                 start=True,
                 stop=True,
@@ -151,15 +135,13 @@ def tile_picked_idxput_add_po_kernel(
         def store(t):
             nc.sync.dma_start(out_rows[:, t, :], plane[t][:])
 
+        nc.vector.tensor_copy(xw_picked[:], xw[:].bitcast(U32).indirect(offs_t[:]))
         nc.vector.tensor_copy(xs_picked[:], xs[:].indirect(offs_t[:]))
-        nc.vector.tensor_copy(w_dst(0)[:, 0:W_ON_VECTOR], w_src[:, 0:W_ON_VECTOR, :, 0:2])
-        nc.scalar.copy(w_dst(0)[:, W_ON_VECTOR:P], w_src[:, W_ON_VECTOR:P, :, 0:2])
-        nc.scalar.copy(w_dst(1), w_src[:, :, :, 2:4])
+        for pair, cut in enumerate(W_ON_VECTOR):
+            planes = slice(2 * pair, 2 * pair + 2)
+            nc.vector.tensor_copy(w_dst(pair)[:, 0:cut], w_src[:, 0:cut, :, planes])
+            nc.scalar.copy(w_dst(pair)[:, cut:P], w_src[:, cut:P, :, planes])
         quantise_w(0)
-        for h in range(2):
-            nc.vector.tensor_copy(
-                xw_picked[h][:], xw[:].bitcast(U32).indirect(offs_t[:, h * HALF // 16 : (h + 1) * HALF // 16])
-            )
         quantise_w(1)
         gather(0, 0, 256)
         gather(0, 256, 384)
@@ -172,7 +154,7 @@ def tile_picked_idxput_add_po_kernel(
         gather(2, 384, 512)
         add("acc_z", [(1, 0, 256)])
         add("acc_x", [(1, 256, 512), (2, 0, 128)])
-        add("acc_y", [(2, 128, 256), (2, 256, 384)])
+        add("acc_y", [(2, 128, 384)])
         gather(3, 0, 128)
         gather(3, 128, 384)
         gather(3, 384, 512, True)

@@ -61,6 +61,8 @@ def tile_picked_idxput_add_po_kernel(
         w_codes = [keep.tile([P, 2 * P], U32, name="w_codes%d" % pair, align_bytes=64) for pair in range(2)]
         w_scales = [keep.tile([P, 2 * P], U8, name="w_scales%d" % pair, align_bytes=64) for pair in range(2)]
 
+        y0 = keep.tile([P, S // 2], F32, name="y0", align_bytes=64)
+        acc0 = psum.tile([P, S // 2], F32, name="acc0")
         old = keep.tile([P, PACK * S], F32, name="old", align_bytes=64)
         new = keep.tile([P, PACK * S], F32, name="new", align_bytes=64)
 
@@ -124,10 +126,10 @@ def tile_picked_idxput_add_po_kernel(
             else:
                 nc.scalar.activation(dst, plane[t][:].indirect(offsets(lo, hi)), COPY)
 
-        def scatter(t, lo, hi):
+        def scatter(t, lo, hi, on_vector=False):
             src = new[:, t * S + lo : t * S + hi]
             window = plane[t][:].indirect(offsets(lo, hi))
-            if t % 2 == 0:
+            if on_vector:
                 nc.vector.tensor_copy(window, src)
             else:
                 nc.scalar.activation(window, src, COPY)
@@ -142,35 +144,31 @@ def tile_picked_idxput_add_po_kernel(
             nc.vector.tensor_copy(w_dst(pair)[:, 0:cut], w_src[:, 0:cut, :, planes])
             nc.scalar.copy(w_dst(pair)[:, cut:P], w_src[:, cut:P, :, planes])
         quantise_w(0)
+        gather(0, 0, 256, True)
+        gather(0, 256, 512)
         quantise_w(1)
-        gather(0, 0, 256)
-        gather(0, 256, 384)
-        gather(0, 384, 512, True)
-        add("acc_a", [(0, 0, 256)])
-        add("acc_b", [(0, 384, 512)])
-        scatter(0, 0, 256)
+        project(acc0[:], 0, 0, 256)
+        nc.scalar.copy(y0[:], acc0[:])
+        nc.vector.tensor_tensor(plane[0][:].indirect(offsets(0, 256)), old[:, 0:256], y0[:], ADD)
         gather(1, 0, 512)
+        add("acc_z", [(0, 384, 512), (1, 0, 256), (1, 256, 384)])
         gather(2, 0, 384)
         gather(2, 384, 512)
-        add("acc_z", [(1, 0, 256)])
-        add("acc_x", [(1, 256, 512), (2, 0, 128)])
-        add("acc_y", [(2, 128, 384)])
-        gather(3, 0, 128)
-        gather(3, 128, 384)
-        gather(3, 384, 512, True)
-        add("acc_d", [(0, 256, 384), (3, 0, 128)])
+        add("acc_y", [(0, 256, 384), (2, 256, 384)])
+        add("acc_x", [(1, 384, 512), (2, 0, 256)])
+        gather(3, 0, 512)
         scatter(1, 256, 512)
-        scatter(0, 256, 512)
+        scatter(0, 256, 512, True)
         store(0)
-        scatter(3, 0, 128)
-        add("acc_r", [(2, 384, 512), (3, 128, 256)])
+        add("acc_v", [(2, 384, 512), (3, 0, 256)])
         add("acc_w", [(3, 256, 512)])
         scatter(1, 0, 256)
         store(1)
-        scatter(2, 0, 512)
-        store(2)
+        scatter(3, 0, 128, True)
+        scatter(2, 0, 512, True)
         scatter(3, 128, 512)
         store(3)
+        store(2)
 
         pairs = keep.tile([P, 2 * U * 2], BF16, name="pairs", align_bytes=64)
         by_pair = pairs[:].rearrange("p (u c e) -> p u c e", u=2, e=2)
@@ -178,13 +176,11 @@ def tile_picked_idxput_add_po_kernel(
 
         for t in range(2):
             nc.gpsimd.tensor_scalar(by_pair[:, 0, :, t], plane[t][:], 1.0, 0.0, MULT, ADD)
-        nc.vector.tensor_copy(
-            by_pair[:, 1, 2 * CHUNK : U, :], plane[2][:, 2 * CHUNK : U].unsqueeze(2).to_broadcast([P, 2 * CHUNK, 2])
-        )
-        nc.vector.tensor_copy(by_pair[:, 1, 0 : 2 * CHUNK, 0], plane[2][:, 0 : 2 * CHUNK])
+        nc.vector.tensor_copy(by_pair[:, 1, 0 : 2 * CHUNK, 1], plane[3][:, 0 : 2 * CHUNK])
+        nc.scalar.copy(by_pair[:, 1, 2 * CHUNK : U, 1], plane[3][:, 2 * CHUNK : U])
         for c in range(2):
-            nc.vector.tensor_copy(by_pair[:, 1, chunks[c], 1], plane[3][:, chunks[c]])
-            nc.scalar.copy(by_pair[:, 1, chunks[2 + c], 1], plane[3][:, chunks[2 + c]])
+            nc.vector.tensor_copy(by_pair[:, 1, chunks[c], 0], plane[2][:, chunks[c]])
+            nc.scalar.copy(by_pair[:, 1, chunks[2 + c], 0], plane[2][:, chunks[2 + c]])
 
         def weave(c, on_scalar):
             dt = U32 if on_scalar else I32

from contextlib import ExitStack

import concourse.mybir as mybir

K, T, S, N, U = 512, 1024, 512, 512, 1024
FLOPS = 2 * K * N * S

F32 = mybir.dt.float32
BF16 = mybir.dt.bfloat16
I32 = mybir.dt.int32
U32 = mybir.dt.uint32
U16 = mybir.dt.uint16
U8 = mybir.dt.uint8
FP8X4 = mybir.dt.float8_e4m3fn_x4
ADD = mybir.AluOpType.add
MULT = mybir.AluOpType.mult
COPY = mybir.ActivationFunctionType.Copy

P = 128
PACK = 4
SCALE_ROWS = 4
CHUNK = U // 4
W_ON_VECTOR = (84, 72)


def tile_picked_idxput_add_po_kernel(
    tc, x_words, x_scales, mem, w1, offs, slot, out_0, out_1, out_2
):
    nc = tc.nc
    with ExitStack() as ctx:
        keep = ctx.enter_context(tc.tile_pool(name="keep", bufs=1))
        psum = ctx.enter_context(tc.psum_pool(name="psum", bufs=1))

        offs_t = keep.tile([P, S // 16], U16, name="offs_t")
        slot_t = keep.tile([P, S // 16], U16, name="slot_t")
        xw = keep.tile([P, T], I32, name="xw", align_bytes=64)
        xs = keep.tile([P, T], U8, name="xs", align_bytes=64)
        w_raw = keep.tile([P, PACK, N], F32, name="w_raw", align_bytes=64)
        plane = [keep.tile([P, U], F32, name="plane%d" % t, align_bytes=64) for t in range(PACK)]
        warm_in = keep.tile([P, 8], F32, name="warm_in")
        warm_out = keep.tile([P, 8], F32, name="warm_out")

        mem_rows = mem.rearrange("(p t) u -> p t u", t=PACK)
        out_rows = out_0.rearrange("(p t) u -> p t u", t=PACK)

        nc.vector.memset(xs[:].bitcast(I32), 0)
        nc.sync.dma_start(xw[:], x_words[0].rearrange("p c r -> p (c r)").bitcast(I32))
        nc.sync.dma_start(offs_t[:], offs)
        for r in range(SCALE_ROWS):
            nc.sync.dma_start(xs[r:P:32, :].bitcast(I32), x_scales[0, r : 16 : SCALE_ROWS, :].bitcast(I32))
        nc.sync.dma_start(slot_t[:], slot)
        nc.vector.memset(warm_in[:], 0.0)
        nc.scalar.copy(warm_out[:], warm_in[:])
        nc.sync.dma_start(w_raw[:], w1.rearrange("(p j) m -> p j m", j=PACK))
        for t in range(PACK):
            nc.sync.dma_start(plane[t][:], mem_rows[:, t, :])

        xw_picked = keep.tile([P, S], U32, name="xw_picked", align_bytes=64)
        xs_picked = keep.tile([P, S], U8, name="xs_picked", align_bytes=64)
        w_bf = [keep.tile([P, 2 * P * PACK], BF16, name="w_bf%d" % pair, align_bytes=64) for pair in range(2)]
        w_codes = [keep.tile([P, 2 * P], U32, name="w_codes%d" % pair, align_bytes=64) for pair in range(2)]
        w_scales = [keep.tile([P, 2 * P], U8, name="w_scales%d" % pair, align_bytes=64) for pair in range(2)]

        y0 = keep.tile([P, S // 2], F32, name="y0", align_bytes=64)
        acc0 = psum.tile([P, S // 2], F32, name="acc0")
        old = keep.tile([P, PACK * S], F32, name="old", align_bytes=64)
        new = keep.tile([P, PACK * S], F32, name="new", align_bytes=64)

        codes = keep.tile([P, U], I32, name="codes", align_bytes=64)
        scales = keep.tile([P, U], U8, name="scales", align_bytes=64)
        grouped = [keep.tile([P, CHUNK * PACK], BF16, name="grouped%d" % c, align_bytes=64) for c in range(4)]

        w_src = w_raw[:].rearrange("p j (m t) -> p m j t", t=PACK)

        def w_dst(pair):
            return w_bf[pair][:].rearrange("p (t m j) -> p m j t", t=2, j=PACK)

        def quantise_w(pair):
            nc.vector.quantize_mx(out=w_codes[pair][:].bitcast(FP8X4), scales=w_scales[pair][:], in_=w_bf[pair][:])

        def offsets(lo, hi):
            return slot_t[:, lo // 16 : hi // 16]

        def project(out, t, lo, hi):
            pair, e = divmod(t, 2)
            cols = slice(e * P, (e + 1) * P)
            nc.tensor.matmul_mx(
                out=out,
                lhsT=w_codes[pair][:, cols].bitcast(FP8X4),
                lhsT_scale=w_scales[pair][:, cols],
                rhs=xw_picked[:, lo:hi].bitcast(FP8X4),
                rhs_scale=xs_picked[:, lo:hi],
                start=True,
                stop=True,
            )

        def add(name, pieces):
            width = sum(hi - lo for t, lo, hi in pieces)
            bank = psum.tile([P, width], F32, name=name)
            at = 0
            for t, lo, hi in pieces:
                project(bank[:, at : at + hi - lo], t, lo, hi)
                at = at + hi - lo
            first, last = (t * S + lo for t, lo, hi in (pieces[0], pieces[min(1, len(pieces) - 1)]))
            step = last - first
            if step < width:
                cols = slice(first, first + width)
                nc.vector.tensor_tensor(new[:, cols], bank[:], old[:, cols], ADD)
                return
            if width == 2 * P:
                dst, src = (
                    x[:].rearrange("p (b c) -> p b c", c=P)[:, first // P : last // P + 1 : step // P, :]
                    for x in (new, old)
                )
            else:
                dst, src = (
                    x[:, first : first + 2 * step].rearrange("p (s c) -> p s c", s=2)[:, :, 0 : width // 2]
                    for x in (new, old)
                )
            nc.vector.tensor_tensor(dst, bank[:].rearrange("p (s c) -> p s c", s=2), src, ADD)

        def gather(t, lo, hi, on_vector=False):
            dst = old[:, t * S + lo : t * S + hi]
            if on_vector:
                nc.vector.tensor_copy(dst, plane[t][:].indirect(offsets(lo, hi)))
            else:
                nc.scalar.activation(dst, plane[t][:].indirect(offsets(lo, hi)), COPY)

        def scatter(t, lo, hi, on_vector=False):
            src = new[:, t * S + lo : t * S + hi]
            window = plane[t][:].indirect(offsets(lo, hi))
            if on_vector:
                nc.vector.tensor_copy(window, src)
            else:
                nc.scalar.activation(window, src, COPY)

        def store(t):
            nc.sync.dma_start(out_rows[:, t, :], plane[t][:])

        nc.vector.tensor_copy(xw_picked[:], xw[:].bitcast(U32).indirect(offs_t[:]))
        nc.vector.tensor_copy(xs_picked[:], xs[:].indirect(offs_t[:]))
        for pair, cut in enumerate(W_ON_VECTOR):
            planes = slice(2 * pair, 2 * pair + 2)
            nc.vector.tensor_copy(w_dst(pair)[:, 0:cut], w_src[:, 0:cut, :, planes])
            nc.scalar.copy(w_dst(pair)[:, cut:P], w_src[:, cut:P, :, planes])
        quantise_w(0)
        gather(0, 0, 256, True)
        gather(0, 256, 512)
        quantise_w(1)
        project(acc0[:], 0, 0, 256)
        nc.scalar.copy(y0[:], acc0[:])
        nc.vector.tensor_tensor(plane[0][:].indirect(offsets(0, 256)), old[:, 0:256], y0[:], ADD)
        gather(1, 0, 512)
        add("acc_z", [(0, 384, 512), (1, 0, 256), (1, 256, 384)])
        gather(2, 0, 384)
        gather(2, 384, 512)
        add("acc_y", [(0, 256, 384), (2, 256, 384)])
        add("acc_x", [(1, 384, 512), (2, 0, 256)])
        gather(3, 0, 512)
        scatter(1, 256, 512)
        scatter(0, 256, 512, True)
        store(0)
        add("acc_v", [(2, 384, 512), (3, 0, 256)])
        add("acc_w", [(3, 256, 512)])
        scatter(1, 0, 256)
        store(1)
        scatter(3, 0, 128, True)
        scatter(2, 0, 512, True)
        scatter(3, 128, 512)
        store(3)
        store(2)

        pairs = keep.tile([P, 2 * U * 2], BF16, name="pairs", align_bytes=64)
        by_pair = pairs[:].rearrange("p (u c e) -> p u c e", u=2, e=2)
        chunks = [slice(c * CHUNK, (c + 1) * CHUNK) for c in range(4)]

        for t in range(2):
            nc.gpsimd.tensor_scalar(by_pair[:, 0, :, t], plane[t][:], 1.0, 0.0, MULT, ADD)
        nc.vector.tensor_copy(by_pair[:, 1, 0 : 2 * CHUNK, 1], plane[3][:, 0 : 2 * CHUNK])
        nc.scalar.copy(by_pair[:, 1, 2 * CHUNK : U, 1], plane[3][:, 2 * CHUNK : U])
        for c in range(2):
            nc.vector.tensor_copy(by_pair[:, 1, chunks[c], 0], plane[2][:, chunks[c]])
            nc.scalar.copy(by_pair[:, 1, chunks[2 + c], 0], plane[2][:, chunks[2 + c]])

        def weave(c, on_scalar):
            dt = U32 if on_scalar else I32
            src = pairs[:].bitcast(dt).rearrange("p (u c) -> p c u", u=2)[:, chunks[c], :]
            dst = grouped[c][:].bitcast(dt).rearrange("p (c u) -> p c u", u=2)
            if on_scalar:
                nc.scalar.copy(dst, src)
            else:
                nc.vector.tensor_copy(dst, src)

        def quantise_result(c):
            cols = slice(c * CHUNK, (c + 1) * CHUNK)
            nc.vector.quantize_mx(out=codes[:, cols].bitcast(FP8X4), scales=scales[:, cols], in_=grouped[c][:])

        words_out = out_1[0].rearrange("p c r -> p (c r)").bitcast(I32)
        weave(0, False)
        weave(2, True)
        weave(3, True)
        weave(1, False)
        quantise_result(0)
        nc.sync.dma_start(words_out[:, 0:CHUNK], codes[:, 0:CHUNK])
        quantise_result(1)
        quantise_result(2)
        nc.sync.dma_start(words_out[:, CHUNK : 3 * CHUNK], codes[:, CHUNK : 3 * CHUNK])
        quantise_result(3)
        nc.scalar.dma_start(words_out[:, 3 * CHUNK :], codes[:, 3 * CHUNK :])
        for r in range(SCALE_ROWS):
            queue = nc.scalar if r == SCALE_ROWS - 1 else nc.sync
            queue.dma_start(out_2[0, r : 16 : SCALE_ROWS, :].bitcast(I32), scales[r:P:32, :].bitcast(I32))
